import numpy as np
import ml_dtypes


def mxq(x, axis, fmt="e4m3"):
    dtype, down = {"e4m3": (ml_dtypes.float8_e4m3fn, 7), "e5m2": (ml_dtypes.float8_e5m2, 14)}[fmt]
    v = np.moveaxis(np.asarray(x, np.float32).astype(ml_dtypes.bfloat16).astype(np.float64), axis, -1)
    blocks = v.reshape(v.shape[:-1] + (-1, 32))
    amax = np.abs(blocks).max(-1, keepdims=True)
    byte = np.maximum(np.where(amax > 0, np.frexp(amax)[1] - 1 + 127, 0) - down, 1)
    scale = np.exp2(byte - 127.0)
    codes = (blocks / scale).astype(np.float32).astype(dtype).astype(np.float64)
    return np.moveaxis((codes * scale).reshape(v.shape), -1, axis)


WIDE = False


def mx_kscale(k):
    if not WIDE:
        return np.ones(k)
    levels = np.array([10, -10, 5, -5, 0])
    if k % 512:
        return np.exp2(np.random.permutation(np.resize(levels, k // 32))).repeat(32)
    a = np.empty((k // 512, 16))
    for p in range(k // 512):
        a[p, :8] = np.random.permutation(np.resize(levels, 8))
        for g in range(8):
            far = levels[np.abs(levels - a[p, g]) >= 10]
            a[p, g + 8] = far[np.random.randint(len(far))]
    return np.exp2(a.ravel()).repeat(32)


BF16 = ml_dtypes.bfloat16


def bf(x):
    return np.asarray(x, np.float32).astype(BF16)


def f64(x):
    return np.asarray(x).astype(np.float64)

def planes(Y):
    n, m = Y.shape
    b = f64(bf(Y)).reshape(n // 32, 32, m)
    amax = np.abs(b).max(1)
    byte = np.clip(np.where(amax > 0, np.frexp(amax)[1] - 1 + 127 - 7, 1), 1, 254)
    codes = (b * np.exp2(127.0 - byte)[:, None, :]).reshape(n, m).astype(np.float32).astype(ml_dtypes.float8_e4m3fn).view(np.uint8)
    words = codes.reshape(n // 512, 128, 4, m).transpose(0, 1, 3, 2)
    return np.ascontiguousarray(words), np.ascontiguousarray(byte.astype(np.uint8).reshape(n // 512, 16, m))


H, TQ, TK, E, DV, M = 2, 1024, 1024, 512, 512, 3


def coef_draw():
    sign = np.where(np.random.uniform(0.0, 1.0, (H, M)) < 0.5, -1.0, 1.0)
    return sign * np.random.uniform(0.4, 1.0, (H, M))


def setup_inputs():
    s, t = mx_kscale(E), mx_kscale(TK)
    return {
        "q": bf(np.random.standard_normal((H, TQ, E)) * s),
        "k": bf(np.random.standard_normal((H, TK, E)) / s),
        "v": bf(np.random.standard_normal((H, TK, DV)) / t[:, None]),
        "ca": bf(coef_draw()),
        "cb": bf(coef_draw()),
        "g": bf((1.0 + 0.1 * np.random.standard_normal((H, TK))) * t),
    }


def fourier_map(s, ca, cb):
    a = np.zeros_like(s)
    for i in range(ca.shape[1]):
        ms = float(i + 1) * s
        cos_coef = ca[:, i][:, None, None]
        sin_coef = cb[:, i][:, None, None]
        a = a + (cos_coef * np.cos(ms) + sin_coef * np.sin(ms))
    return a


def core(q, k, v, ca, cb, g):
    t = k.shape[1]
    e = q.shape[2]
    qq = mxq(f64(q), 2, "e4m3")
    kq = mxq(f64(k), 2, "e4m3")
    s = (qq @ kq.transpose(0, 2, 1)) / np.sqrt(e)
    a = fourier_map(s, f64(ca), f64(cb))
    ag = a * f64(g)[:, None, :]
    return (mxq(ag, 2, "e4m3") @ mxq(f64(v), 1, "e4m3")) / np.sqrt(t)


def reference(q, k, v, ca, cb, g):
    R_out = core(q, k, v, ca, cb, g)
    words, scales = planes(np.moveaxis(R_out, 1, 0).reshape(1024, -1))
    return R_out, words, scales

@@ -1,0 +1,485 @@
+import math
+from contextlib import ExitStack
+
+import concourse.mybir as mybir
+from concourse.masks import make_identity
+
+H, TQ, TK, E, DV = 2, 1024, 1024, 512, 512
+FLOPS = 2 * H * TQ * TK * (E + DV)
+
+F32 = mybir.dt.float32
+BF16 = mybir.dt.bfloat16
+I32 = mybir.dt.int32
+U32 = mybir.dt.uint32
+U8 = mybir.dt.uint8
+FP8X4 = mybir.dt.float8_e4m3fn_x4
+ALU = mybir.AluOpType
+ACT = mybir.ActivationFunctionType
+AX = mybir.AxisListType
+
+P = 128
+PACK = 4
+GROUP = P * PACK
+UNITS = H * TQ // P
+PI = math.pi
+TURNS = 1.0 / (2.0 * PI * math.sqrt(E))
+TINY = 1e-37
+
+
+def tile_fourierkolmogorovarnoldattention_x1_kernel(tc, q, k, v, ca, cb, g, out_0, out_1, out_2):
+    nc = tc.nc
+    with ExitStack() as ctx:
+        keep = ctx.enter_context(tc.tile_pool(name="keep", bufs=1))
+        work = ctx.enter_context(tc.tile_pool(name="work", bufs=2))
+        psum = ctx.enter_context(tc.psum_pool(name="psum", bufs=1))
+        ctx.enter_context(tc.manual_schedule())
+
+        ca_sb = keep.tile([P, H, 3], BF16, name="ca_sb")
+        cb_sb = keep.tile([P, H, 3], BF16, name="cb_sb")
+        g_sb = keep.tile([P, H * 2, PACK], BF16, name="g_sb")
+        nc.sync.dma_start(out=ca_sb[:].rearrange("p h m -> p (h m)"),
+                          in_=ca.rearrange("h m -> (h m)").partition_broadcast(P))
+        nc.sync.dma_start(out=cb_sb[:].rearrange("p h m -> p (h m)"),
+                          in_=cb.rearrange("h m -> (h m)").partition_broadcast(P))
+        raw = {}
+
+        def load(name, src, h, half):
+            t = keep.tile([P, PACK, 512], BF16, name="raw_%s%d%d" % (name, h, half), align_bytes=64)
+            nc.sync.dma_start(out=t[:], in_=src[h, half * GROUP:(half + 1) * GROUP, :].rearrange("(p j) e -> p j e", j=PACK))
+            raw[(name, h, half)] = t
+
+        load("k", k, 0, 0)
+        load("q", q, 0, 0)
+        load("k", k, 0, 1)
+        nc.sync.dma_start(out=g_sb[:], in_=g.rearrange("h (kk p j) -> p (h kk) j", p=P, j=PACK))
+        load("v", v, 0, 0)
+        load("v", v, 0, 1)
+        load("q", q, 0, 1)
+        load("k", k, 1, 0)
+        load("k", k, 1, 1)
+        load("q", q, 1, 0)
+        load("v", v, 1, 0)
+        load("v", v, 1, 1)
+        load("q", q, 1, 1)
+
+        ident = keep.tile([P, P], F32, name="ident")
+        make_identity(nc, ident[:])
+        half_t = keep.tile([P, H], F32, name="half_t")
+        nc.gpsimd.memset(half_t[:], 0.5)
+
+        codes = {}
+        scales = {}
+        for name in ("q", "k", "v"):
+            for h in range(H):
+                codes[(name, h)] = keep.tile([P, 1024], U32, name="codes_%s%d" % (name, h), align_bytes=64)
+                scales[(name, h)] = keep.tile([P, 1024], U8, name="scales_%s%d" % (name, h), align_bytes=64)
+
+        turned = {}
+        grouped = {}
+
+        def prep_transpose(job):
+            name, h, b = job
+            xt = psum.tile([P, 2, 2, P], F32, name="xt", tag="xt", bufs=2)
+            for s in range(2):
+                words = raw[(name, h, b // 2)][:, 2 * (b % 2) + s, :].bitcast(F32)
+                for u in range(2):
+                    nc.tensor.transpose(xt[:, s, u, :], words[:, u:256:2], ident[:])
+            turned[job] = xt
+
+        def prep_copy(job):
+            t = work.tile([P, 1024], BF16, name="grouped", tag="grouped", bufs=3, align_bytes=64)
+            nc.scalar.copy(out=t[:].bitcast(F32).rearrange("p (s r u) -> p s r u", s=2, u=2),
+                           in_=turned[job][:].rearrange("p s u r -> p s r u"))
+            grouped[job] = t
+
+        def prep_quantize(job):
+            name, h, b = job
+            cols = slice(256 * b, 256 * (b + 1))
+            nc.vector.quantize_mx(out=codes[(name, h)][:, cols].bitcast(FP8X4), scales=scales[(name, h)][:, cols],
+                                  in_=grouped[job][:])
+
+        def v_interleave(h, kk, on_vector):
+            t = work.tile([P, 512, PACK], BF16, name="vgrouped", tag="vgrouped", align_bytes=64)
+            src = raw[("v", h, kk)][:].rearrange("p j d -> p d j")
+            if on_vector:
+                nc.vector.tensor_copy(out=t[:], in_=src)
+            else:
+                nc.scalar.copy(out=t[:], in_=src)
+            grouped[("v", h, kk)] = t
+
+        def v_quantize(h, kk):
+            cols = slice(512 * kk, 512 * (kk + 1))
+            nc.vector.quantize_mx(out=codes[("v", h)][:, cols].bitcast(FP8X4), scales=scales[("v", h)][:, cols],
+                                  in_=grouped[("v", h, kk)][:].rearrange("p d j -> p (d j)"))
+
+        def small(name, *shape):
+            return keep.tile([P] + list(shape), F32, name=name)
+
+        def tt(out, a, b, op):
+            nc.vector.tensor_tensor(out=out, in0=a, in1=b, op=op)
+
+        def ts(out, a, s1, op0, s2=None, op1=None):
+            if op1 is None:
+                nc.vector.tensor_scalar(out=out, in0=a, scalar1=s1, scalar2=None, op0=op0)
+            else:
+                nc.vector.tensor_scalar(out=out, in0=a, scalar1=s1, scalar2=s2, op0=op0, op1=op1)
+
+        def stt(out, a, s, op0, b, op1):
+            nc.vector.scalar_tensor_tensor(out=out, in0=a, scalar=s, in1=b, op0=op0, op1=op1)
+
+        def sine(out, a, scale, bias=None):
+            if bias is None:
+                nc.scalar.activation(out=out, in_=a, func=ACT.Sin, scale=scale)
+            else:
+                nc.scalar.activation(out=out, in_=a, func=ACT.Sin, scale=scale, bias=bias)
+
+        mul, add, sub, mx = ALU.mult, ALU.add, ALU.subtract, ALU.max
+        absa = small("absa", H, 3)
+        absb = small("absb", H, 3)
+        m3 = small("m3", H)
+        im3 = small("im3", H)
+        r = small("r", 3, H)
+        cs = small("cs", 2, H)
+        flat_a = ca_sb[:].rearrange("p h m -> p (h m)")
+        flat_b = cb_sb[:].rearrange("p h m -> p (h m)")
+        stt(absa[:].rearrange("p h m -> p (h m)"), flat_a, -1.0, mul, flat_a, mx)
+        stt(absb[:].rearrange("p h m -> p (h m)"), flat_b, -1.0, mul, flat_b, mx)
+        sig0 = small("sig0", H)
+        ts(sig0[:], cb_sb[:, :, 2], 0.0, ALU.is_le, 2.0, mul)
+        stt(m3[:], absb[:, :, 2], TINY, mx, absa[:, :, 2], add)
+        sig = small("sig", H, 1)
+        ts(sig[:, :, 0], sig0[:], -1.0, add)
+        nc.vector.reciprocal(out=im3[:], in_=m3[:])
+        absab = small("absab", H, 3)
+        tt(absab[:], absa[:], absb[:], add)
+        stt(r[:, 0, :], ca_sb[:, :, 2], -1.0, mul, im3[:], mul)
+        stt(r[:, 1, :], absb[:, :, 2], TINY, mx, im3[:], mul)
+        sine(cs[:], r[:, 0:2, :], PI / 2)
+        stt(r[:, 2, :], ca_sb[:, :, 2], -1.0, mul, im3[:], mul)
+        total = small("total", H)
+        nc.vector.tensor_reduce(out=total[:], in_=absab[:], axis=AX.X, op=add)
+        base = small("base", H)
+        ts(base[:], r[:, 0, :], -PI / 6, mul, PI / 6, add)
+        ab = small("ab", 2, H, 2)
+        ba = small("ba", 2, H, 2)
+        nc.vector.tensor_copy(out=ab[:, 0, :, :], in_=ca_sb[:, :, 0:2])
+        nc.vector.tensor_copy(out=ab[:, 1, :, :], in_=cb_sb[:, :, 0:2])
+        tt(ba[:, 0, :, :], cb_sb[:, :, 0:2], sig[:].to_broadcast([P, H, 2]), mul)
+        stt(ba[:, 1, :, :], ca_sb[:, :, 0:2], -1.0, mul, sig[:].to_broadcast([P, H, 2]), mul)
+        floor = small("floor", H)
+        ts(floor[:], total[:], 2.0 ** -40, mul)
+        pr1 = small("pr1", 2, H)
+        pr2 = small("pr2", 2, H)
+        tt(pr1[:], r[:, 0:2, :], cs[:], mul)
+        tt(pr2[:], r[:, 1:3, :], cs[:], mul)
+        den = small("den", H)
+        num = small("num", H)
+        tt(den[:], pr1[:, 0, :], pr1[:, 1, :], add)
+        tt(num[:], pr2[:, 0, :], pr2[:, 1, :], sub)
+        iden = small("iden", H)
+        nc.vector.reciprocal(out=iden[:], in_=den[:])
+        dm = small("dm", H)
+        stt(dm[:], den[:], 32.0, mul, m3[:], mul)
+        z = small("z", H)
+        tt(z[:], num[:], iden[:], mul)
+        w = small("w", H)
+        tt(w[:], z[:], z[:], mul)
+        z3 = small("z3", H)
+        ts(z3[:], z[:], 1.0 / 3.0, mul)
+        p1 = small("p1", H)
+        q1 = small("q1", H)
+        ts(p1[:], w[:], -1.0 / 7.0, mul, 1.0 / 5.0, add)
+        ts(q1[:], w[:], 1.0 / 16.0, mul, -1.0 / 8.0, add)
+        p2 = small("p2", H)
+        q2 = small("q2", H)
+        tt(p2[:], p1[:], w[:], mul)
+        tt(q2[:], q1[:], w[:], mul)
+        p3 = small("p3", H)
+        q3 = small("q3", H)
+        stt(p3[:], p2[:], -1.0 / 3.0, add, w[:], mul)
+        stt(q3[:], q2[:], 0.5, add, w[:], mul)
+        e3 = small("e3", H)
+        r32 = small("r32", H)
+        stt(e3[:], p3[:], 1.0, add, z3[:], mul)
+        stt(r32[:], q3[:], 1.0, add, dm[:], mul)
+        pa = small("pa", H)
+        tt(pa[:], e3[:], base[:], add)
+        cosm = small("cosm", 1, H, 2)
+        sinm = small("sinm", 1, H, 2)
+        sine(cosm[:, 0, :, 0], pa[:], -1.0, PI / 2)
+        sine(cosm[:, 0, :, 1], pa[:], -2.0, PI / 2)
+        sine(sinm[:, 0, :, 0], pa[:], 1.0)
+        sine(sinm[:, 0, :, 1], pa[:], 2.0)
+        big_k = small("big_k", H, 1)
+        tt(big_k[:, :, 0], r32[:], floor[:], mx)
+        phi = small("phi", H)
+        tt(phi[:], pa[:], sig[:, :, 0], mul)
+        ik = small("ik", H, 1)
+        nc.vector.reciprocal(out=ik[:, :, 0], in_=big_k[:, :, 0])
+        phit = small("phit", H)
+        ts(phit[:], phi[:], 1.0 / (2 * PI), mul)
+        xb = small("xb", H)
+        ts(xb[:], phi[:], -0.5, mul)
+
+        prologue = [("k", 0, 0), ("k", 0, 1), ("q", 0, 0), ("k", 0, 2), ("k", 0, 3), ("q", 0, 1)]
+        prep_transpose(prologue[0])
+        prep_copy(prologue[0])
+        prep_transpose(prologue[1])
+
+        rc = small("rc", 2, H * 2)
+        rs = small("rs", 2, H * 2)
+        tt(rc[:], ab[:].rearrange("p a h m -> p a (h m)"),
+           cosm[:].rearrange("p a h m -> p a (h m)").to_broadcast([P, 2, H * 2]), mul)
+        tt(rs[:], ba[:].rearrange("p a h m -> p a (h m)"),
+           sinm[:].rearrange("p a h m -> p a (h m)").to_broadcast([P, 2, H * 2]), mul)
+        rot = small("rot", 2, H, 2)
+        tt(rot[:].rearrange("p a h m -> p a (h m)"), rc[:], rs[:], add)
+        absr = small("absr", H, 2)
+        stt(absr[:], rot[:, 1, :, :], -1.0, mul, rot[:, 1, :, :], mx)
+        ak = small("ak", H, 2)
+        tt(ak[:], rot[:, 0, :, :], ik[:].to_broadcast([P, H, 2]), mul)
+        mm = small("mm", H)
+        stt(mm[:], absr[:, :, 1], TINY, mx, absr[:, :, 0], add)
+        nm = small("nm", 2, H)
+        tt(nm[:, 1, :], rot[:, 1, :, 0], ik[:, :, 0], mul)
+        imm = small("imm", H)
+        nc.vector.reciprocal(out=imm[:], in_=mm[:])
+        mk = small("mk", H)
+        stt(mk[:], mm[:], 2.0, mul, ik[:, :, 0], mul)
+        rho = small("rho", H)
+        ar = small("ar", H)
+        tt(rho[:], rot[:, 1, :, 1], imm[:], mul)
+        tt(ar[:], absr[:, :, 1], imm[:], mul)
+        psit = small("psit", H)
+        stt(psit[:], rho[:], 1.0 / 8.0, mul, phit[:], sub)
+        zr = small("zr", H)
+        ts(zr[:], ar[:], 1e-4, mx)
+        psir = small("psir", H)
+        stt(psir[:], rho[:], PI / 4, mul, phi[:], sub)
+        dn = small("dn", 2, H)
+        sd = small("sd", H)
+        c2d = small("c2d", H)
+        sine(dn[:, 1, :], rho[:], PI / 4, PI / 2)
+        sine(sd[:], rho[:], PI / 4)
+        sine(c2d[:], ar[:], -PI / 2, PI / 2)
+        sine(dn[:, 0, :], zr[:], PI / 2)
+        tt(nm[:, 0, :], mk[:], zr[:], mul)
+
+        prep_copy(prologue[1])
+        prep_quantize(prologue[0])
+        prep_transpose(prologue[2])
+        prep_copy(prologue[2])
+        prep_transpose(prologue[3])
+
+        idn = small("idn", 2, H)
+        nc.vector.reciprocal(out=idn[:], in_=dn[:])
+        prep_quantize(prologue[1])
+        ml = small("ml", 2, H)
+        tt(ml[:], nm[:], idn[:], mul)
+        al = small("al", H)
+        nc.gpsimd.tensor_tensor(out=al[:], in0=ml[:, 0, :], in1=half_t[:], op=ALU.pow)
+        gk = small("gk", H * 2, 1, PACK)
+        tt(gk[:].rearrange("p (h kk) o j -> p h (kk o j)", h=H), g_sb[:].rearrange("p (h kk) j -> p h (kk j)", h=H),
+           big_k[:].to_broadcast([P, H, 2 * PACK]), mul)
+        t_a2 = small("t_a2", H)
+        t_a1 = small("t_a1", H)
+        stt(t_a2[:], ml[:, 0, :], 0.5, mul, c2d[:], mul)
+        tt(t_a1[:], ml[:, 1, :], sd[:], mul)
+        a2 = small("a2", H)
+        a1 = small("a1", H)
+        tt(a2[:], t_a2[:], ak[:, :, 1], add)
+        tt(a1[:], ak[:, :, 0], t_a1[:], sub)
+
+        prep_copy(prologue[3])
+        prep_quantize(prologue[2])
+        prep_transpose(prologue[4])
+        prep_copy(prologue[4])
+        prep_transpose(prologue[5])
+
+        c_a = small("c_a", H)
+        ts(c_a[:], a2[:], 8.0, mul, -1.5, add)
+        b0 = small("b0", H)
+        stt(b0[:], a2[:], 4.0, mul, a1[:], add)
+        e0 = small("e0", H)
+        stt(e0[:], a2[:], -1.0 / 32.0, add, a1[:], add)
+        ial = small("ial", H)
+        nc.vector.reciprocal(out=ial[:], in_=al[:])
+        c_b = small("c_b", H)
+        ts(c_b[:], b0[:], -2.0, mul, 9.0 / 16.0, add)
+        be = small("be", H)
+        stt(be[:], ml[:, 1, :], 0.5, mul, ial[:], mul)
+        e1 = small("e1", H)
+        stt(e1[:], ml[:, 0, :], -0.5, mul, e0[:], add)
+        be2 = small("be2", H)
+        tt(be2[:], be[:], be[:], mul)
+        prep_quantize(prologue[3])
+        c_e = small("c_e", H)
+        tt(c_e[:], e1[:], be2[:], sub)
+        prep_quantize(prologue[4])
+        prep_copy(prologue[5])
+
+        s_ps, frac, u_t, tb_t, t2_t, ta_t, z_ps, ag_t, agq, o_ps, o_sb, o_bf = ({} for n in range(12))
+
+        def head(i):
+            return i // 8
+
+        def scores(i):
+            h = head(i)
+            qcols = slice(P * (i % 8), P * (i % 8 + 1))
+            for kk in range(2):
+                bank = psum.tile([P, 512], F32, name="s_ps", tag="s%d" % kk)
+                kcols = slice(512 * kk, 512 * (kk + 1))
+                nc.tensor.matmul_mx(out=bank[:], lhsT=codes[("q", h)][:, qcols].bitcast(FP8X4),
+                                    lhsT_scale=scales[("q", h)][:, qcols],
+                                    rhs=codes[("k", h)][:, kcols].bitcast(FP8X4), rhs_scale=scales[("k", h)][:, kcols],
+                                    start=True, stop=True)
+                s_ps[(i, kk)] = bank
+
+        def reduce_angle(i):
+            h = head(i)
+            whole = work.tile([P, 2, 512], I32, name="whole", tag="whole")
+            f = work.tile([P, 2, 512], F32, name="frac", tag="frac")
+            for kk in range(2):
+                ts(whole[:, kk, :], s_ps[(i, kk)][:], TURNS, mul, psit[:, h:h + 1], add)
+            for kk in range(2):
+                stt(f[:, kk, :], s_ps[(i, kk)][:], TURNS, mul, whole[:, kk, :], sub)
+            frac[i] = f
+
+        def sines(i):
+            h = head(i)
+            f = frac[i][:].rearrange("p a n -> p (a n)")
+            x = work.tile([P, 1024], F32, name="x", tag="x")
+            sn = work.tile([P, 1024], F32, name="sn", tag="sn")
+            u = work.tile([P, 1024], F32, name="u", tag="u")
+            tb = work.tile([P, 1024], F32, name="tb", tag="tb")
+            sine(x[:], f, PI, xb[:, h:h + 1])
+            sine(sn[:], f, 2 * PI, psir[:, h:h + 1])
+            nc.scalar.activation(out=u[:], in_=x[:], func=ACT.Square)
+            nc.scalar.activation(out=tb[:], in_=sn[:], func=ACT.Square, scale=al[:, h:h + 1], bias=be[:, h:h + 1])
+            u_t[i], tb_t[i] = u, tb
+
+        def cubic_first(i):
+            h = head(i)
+            t2 = work.tile([P, 1024], F32, name="t2", tag="t2")
+            stt(t2[:], u_t[i][:], c_a[:, h:h + 1], add, u_t[i][:], mul)
+            t2_t[i] = t2
+
+        def cubic_second(i):
+            h = head(i)
+            ta = work.tile([P, 1024], F32, name="ta", tag="ta")
+            stt(ta[:], t2_t[i][:], c_b[:, h:h + 1], add, u_t[i][:], mul)
+            ta_t[i] = ta
+
+        def turn_and_add(i):
+            for kk in range(2):
+                bank = psum.tile([P, PACK, P], F32, name="z_ps", tag="z%d" % kk)
+                for j in range(PACK):
+                    cols = slice(512 * kk + P * j, 512 * kk + P * (j + 1))
+                    nc.tensor.matmul(out=bank[:, j, :], lhsT=tb_t[i][:, cols], rhs=ident[:], start=True, stop=False,
+                                     is_transpose=True)
+                    nc.tensor.matmul(out=bank[:, j, :], lhsT=ta_t[i][:, cols], rhs=ident[:], start=False, stop=True,
+                                     is_transpose=True)
+                z_ps[(i, kk)] = bank
+
+        def gain(i):
+            h = head(i)
+            ag = work.tile([P, 2, P, PACK], BF16, name="ag", tag="ag", align_bytes=64)
+            for kk in range(2):
+                stt(ag[:, kk, :, :], z_ps[(i, kk)][:].rearrange("p j n -> p n j"), c_e[:, h:h + 1], add,
+                    gk[:, 2 * h + kk, :, :].to_broadcast([P, P, PACK]), mul)
+            ag_t[i] = ag
+
+        def quantize_ag(i):
+            c = work.tile([P, 2 * P], U32, name="ag_codes", tag="ag_codes", align_bytes=64)
+            s = work.tile([P, 2 * P], U8, name="ag_scales", tag="ag_scales", align_bytes=64)
+            nc.vector.quantize_mx(out=c[:].bitcast(FP8X4), scales=s[:], in_=ag_t[i][:].rearrange("p a n j -> p (a n j)"))
+            agq[i] = (c, s)
+
+        def weighted_sum(i):
+            h = head(i)
+            c, s = agq[i]
+            bank = psum.tile([P, DV], F32, name="o_ps", tag="o", bufs=2)
+            for kk in range(2):
+                acols = slice(P * kk, P * (kk + 1))
+                vcols = slice(512 * kk, 512 * (kk + 1))
+                nc.tensor.matmul_mx(out=bank[:], lhsT=c[:, acols].bitcast(FP8X4), lhsT_scale=s[:, acols],
+                                    rhs=codes[("v", h)][:, vcols].bitcast(FP8X4), rhs_scale=scales[("v", h)][:, vcols],
+                                    start=(kk == 0), stop=(kk == 1))
+            o_ps[i] = bank
+
+        def result(i):
+            grp, t = divmod(i, PACK)
+            h, gq = divmod(grp, 2)
+            if t == 0:
+                o_sb[grp] = work.tile([P, PACK, DV], F32, name="o_sb", tag="o_sb")
+            nc.scalar.mul(out=o_sb[grp][:, t, :], in_=o_ps[i][:], mul=1.0 / math.sqrt(TK))
+            rows = out_0[h, GROUP * gq:GROUP * (gq + 1), :].rearrange("(p t) d -> p t d", t=PACK)
+            nc.sync.dma_start(out=rows[:, t, :], in_=o_sb[grp][:, t, :])
+
+        def round_result(grp, split):
+            o_bf[grp] = work.tile([P, DV, PACK], BF16, name="o_bf", tag="o_bf", align_bytes=64)
+            src = o_sb[grp][:].rearrange("p t d -> p d t")
+            if split > 0:
+                nc.vector.tensor_copy(out=o_bf[grp][:, 0:split, :], in_=src[:, 0:split, :])
+            if split < DV:
+                nc.scalar.copy(out=o_bf[grp][:, split:DV, :], in_=src[:, split:DV, :])
+
+        def planes(grp):
+            h, gq = divmod(grp, 2)
+            c = work.tile([P, DV], U32, name="o_codes", tag="o_codes", align_bytes=64)
+            s = work.tile([P, DV], U8, name="o_scales", tag="o_scales", align_bytes=64)
+            nc.vector.quantize_mx(out=c[:].bitcast(FP8X4), scales=s[:], in_=o_bf[grp][:].rearrange("p d t -> p (d t)"))
+            cols = slice(DV * h, DV * (h + 1))
+            nc.sync.dma_start(out=out_1[gq, :, cols, :].rearrange("p m t -> p (m t)").bitcast(I32), in_=c[:].bitcast(I32))
+            for quad in range(4):
+                nc.sync.dma_start(out=out_2[gq, 4 * quad:4 * quad + 4, cols].bitcast(I32),
+                                  in_=s[32 * quad:32 * quad + 4, :].bitcast(I32))
+
+        jobs = {-2: ("q", 0, 2), -1: ("q", 0, 3), 0: ("k", 1, 0), 1: ("k", 1, 1), 2: ("k", 1, 2), 3: ("k", 1, 3),
+                4: ("q", 1, 0), 5: ("q", 1, 1), 6: ("q", 1, 2), 7: ("q", 1, 3), -3: prologue[5]}
+
+        def live(i):
+            return 0 <= i < UNITS
+
+        scores(0)
+        for i in range(-2, UNITS + 2):
+            if live(i + 1):
+                sines(i + 1)
+            if live(i):
+                cubic_first(i)
+            if live(i - 1):
+                quantize_ag(i - 1)
+                weighted_sum(i - 1)
+            if i - 1 in jobs:
+                prep_quantize(jobs[i - 1])
+            if live(i):
+                cubic_second(i)
+                turn_and_add(i)
+            if live(i + 2):
+                reduce_angle(i + 2)
+            if i in jobs:
+                prep_transpose(jobs[i])
+            if live(i + 3):
+                scores(i + 3)
+            if i == -2:
+                v_interleave(0, 0, True)
+            if i == -1:
+                v_quantize(0, 0)
+                v_interleave(0, 1, True)
+            if i == 0:
+                v_quantize(0, 1)
+            if i in (7, 8):
+                v_quantize(1, i - 7)
+            if i >= 2 and (i - 2) % PACK == 0 and i > 2:
+                planes((i - 2) // PACK - 1)
+            if live(i - 1):
+                result(i - 1)
+            if i in jobs:
+                prep_copy(jobs[i])
+            if i in (6, 7):
+                v_interleave(1, i - 6, False)
+            if live(i):
+                gain(i)
+            if i >= PACK and i % PACK == 0:
+                round_result(i // PACK - 1, 1280 // PACK if i == UNITS else 0)
+        planes(3)

@@ -24,6 +24,16 @@ UNITS = H * TQ // P
 PI = math.pi
 TURNS = 1.0 / (2.0 * PI * math.sqrt(E))
 TINY = 1e-37
+MODES = "ACCCCCCCCCCCCCDA"
+U_PARTS = ((0, 1024),)
+WARM = (0, 0)
+AV_START = 2
+V0_HEAD = 4
+FILL_ON = "VAA"
+PREP_ON = "AAAAAAAA"
+V0_PLAN = ((0, "L"), (0, "L"), (1, "L"), (1, "V"), 2)
+V1_PLAN = ((2, "V"), (3, "V"), (3, "V"), (4, "V"), (4, "V"), (5, "V"), (5, "V"), (6, "V"), 7, 8)
+CAST_PLAN = (((7, "V"), (8, "V"), (8, "L"), (9, "V"), 10), ((9, "L"), (10, "L"), (11, "V"), (11, "V"), 12), ((12, "L"), (13, "V"), (13, "L"), (13, "V"), 14))
 
 
 def tile_fourierkolmogorovarnoldattention_x1_kernel(tc, q, k, v, ca, cb, g, out_0, out_1, out_2):
@@ -43,23 +53,26 @@ def tile_fourierkolmogorovarnoldattention_x1_kernel(tc, q, k, v, ca, cb, g, out_
                           in_=cb.rearrange("h m -> (h m)").partition_broadcast(P))
         raw = {}
 
-        def load(name, src, h, half):
-            t = keep.tile([P, PACK, 512], BF16, name="raw_%s%d%d" % (name, h, half), align_bytes=64)
-            nc.sync.dma_start(out=t[:], in_=src[h, half * GROUP:(half + 1) * GROUP, :].rearrange("(p j) e -> p j e", j=PACK))
-            raw[(name, h, half)] = t
+        def load(name, src, h, half, lo=0, hi=PACK):
+            if lo == 0:
+                raw[(name, h, half)] = keep.tile([P, PACK, 512], BF16, name="raw_%s%d%d" % (name, h, half), align_bytes=64)
+            rows = src[h, half * GROUP:(half + 1) * GROUP, :].rearrange("(p j) e -> p j e", j=PACK)
+            nc.sync.dma_start(out=raw[(name, h, half)][:, lo:hi, :], in_=rows[:, lo:hi, :])
 
-        load("k", k, 0, 0)
-        load("q", q, 0, 0)
+        load("k", k, 0, 0, 0, 2)
+        load("k", k, 0, 0, 2, 4)
+        load("q", q, 0, 0, 0, 2)
         load("k", k, 0, 1)
-        nc.sync.dma_start(out=g_sb[:], in_=g.rearrange("h (kk p j) -> p (h kk) j", p=P, j=PACK))
+        load("q", q, 0, 0, 2, 4)
         load("v", v, 0, 0)
-        load("v", v, 0, 1)
+        nc.sync.dma_start(out=g_sb[:], in_=g.rearrange("h (kk p j) -> p (h kk) j", p=P, j=PACK))
         load("q", q, 0, 1)
+        load("v", v, 0, 1)
         load("k", k, 1, 0)
-        load("k", k, 1, 1)
-        load("q", q, 1, 0)
         load("v", v, 1, 0)
+        load("k", k, 1, 1)
         load("v", v, 1, 1)
+        load("q", q, 1, 0)
         load("q", q, 1, 1)
 
         ident = keep.tile([P, P], F32, name="ident")
@@ -74,22 +87,30 @@ def tile_fourierkolmogorovarnoldattention_x1_kernel(tc, q, k, v, ca, cb, g, out_
                 codes[(name, h)] = keep.tile([P, 1024], U32, name="codes_%s%d" % (name, h), align_bytes=64)
                 scales[(name, h)] = keep.tile([P, 1024], U8, name="scales_%s%d" % (name, h), align_bytes=64)
 
+        def copy(eng, out, in_):
+            if eng in "AL":
+                nc.scalar.copy(out=out, in_=in_)
+            elif eng == "V":
+                nc.vector.tensor_copy(out=out, in_=in_)
+            else:
+                nc.gpsimd.tensor_scalar(out=out, in0=in_, scalar1=1.0, scalar2=0.0, op0=ALU.mult, op1=ALU.add)
+
         turned = {}
         grouped = {}
 
-        def prep_transpose(job):
+        def prep_transpose(job, tag="xt", bufs=2):
             name, h, b = job
-            xt = psum.tile([P, 2, 2, P], F32, name="xt", tag="xt", bufs=2)
+            xt = psum.tile([P, 2, 2, P], F32, name="xt", tag=tag, bufs=bufs)
             for s in range(2):
                 words = raw[(name, h, b // 2)][:, 2 * (b % 2) + s, :].bitcast(F32)
                 for u in range(2):
                     nc.tensor.transpose(xt[:, s, u, :], words[:, u:256:2], ident[:])
             turned[job] = xt
 
-        def prep_copy(job):
-            t = work.tile([P, 1024], BF16, name="grouped", tag="grouped", bufs=3, align_bytes=64)
-            nc.scalar.copy(out=t[:].bitcast(F32).rearrange("p (s r u) -> p s r u", s=2, u=2),
-                           in_=turned[job][:].rearrange("p s u r -> p s r u"))
+        def prep_copy(job, eng):
+            t = work.tile([P, 1024], BF16, name="grouped", tag="grouped", bufs=4, align_bytes=64)
+            copy(eng, t[:].bitcast(F32).rearrange("p (s r u) -> p s r u", s=2, u=2),
+                 turned[job][:].rearrange("p s u r -> p s r u"))
             grouped[job] = t
 
         def prep_quantize(job):
@@ -98,14 +119,11 @@ def tile_fourierkolmogorovarnoldattention_x1_kernel(tc, q, k, v, ca, cb, g, out_
             nc.vector.quantize_mx(out=codes[(name, h)][:, cols].bitcast(FP8X4), scales=scales[(name, h)][:, cols],
                                   in_=grouped[job][:])
 
-        def v_interleave(h, kk, on_vector):
-            t = work.tile([P, 512, PACK], BF16, name="vgrouped", tag="vgrouped", align_bytes=64)
-            src = raw[("v", h, kk)][:].rearrange("p j d -> p d j")
-            if on_vector:
-                nc.vector.tensor_copy(out=t[:], in_=src)
-            else:
-                nc.scalar.copy(out=t[:], in_=src)
-            grouped[("v", h, kk)] = t
+        def v_interleave(h, kk, part, eng):
+            if part == 0:
+                grouped[("v", h, kk)] = work.tile([P, 512, PACK], BF16, name="vgrouped", tag="vgrouped", align_bytes=64)
+            cols = slice(128 * part, 128 * (part + 1))
+            copy(eng, grouped[("v", h, kk)][:, cols, :], raw[("v", h, kk)][:].rearrange("p j d -> p d j")[:, cols, :])
 
         def v_quantize(h, kk):
             cols = slice(512 * kk, 512 * (kk + 1))
@@ -134,6 +152,180 @@ def tile_fourierkolmogorovarnoldattention_x1_kernel(tc, q, k, v, ca, cb, g, out_
                 nc.scalar.activation(out=out, in_=a, func=ACT.Sin, scale=scale, bias=bias)
 
         mul, add, sub, mx = ALU.mult, ALU.add, ALU.subtract, ALU.max
+        al = small("al", H)
+        be = small("be", H)
+        nus = small("nus", H)
+        nk = small("nk", H)
+        c_a = small("c_a", H)
+        c_b = small("c_b", H)
+        c_e = small("c_e", H)
+        c_e2 = small("c_e2", H)
+        xb = small("xb", H)
+        psit = small("psit", H)
+        psir = small("psir", H)
+        gk = small("gk", H * 2, 1, PACK)
+
+        s_ps, whole_t, frac, x_t, u_t, y_t, tb_t, ta_t, z_ps, ag_t, agq, o_ps, o_sb, o_bf, o_q = ({} for n in range(15))
+
+        def head(i):
+            return i // 8
+
+        def scores(i, kk):
+            h = head(i)
+            qcols = slice(P * (i % 8), P * (i % 8 + 1))
+            bank = psum.tile([P, 512], F32, name="s_ps", tag="s%d" % kk)
+            kcols = slice(512 * kk, 512 * (kk + 1))
+            nc.tensor.matmul_mx(out=bank[:], lhsT=codes[("q", h)][:, qcols].bitcast(FP8X4),
+                                lhsT_scale=scales[("q", h)][:, qcols],
+                                rhs=codes[("k", h)][:, kcols].bitcast(FP8X4), rhs_scale=scales[("k", h)][:, kcols],
+                                start=True, stop=True)
+            s_ps[(i, kk)] = bank
+
+        def out_bank(i):
+            if i not in o_ps:
+                o_ps[i] = psum.tile([P, DV], F32, name="o_ps", tag="o", bufs=2)
+            return o_ps[i]
+
+        def keep_warm(i, n):
+            for rep in range(n):
+                nc.tensor.matmul_mx(out=out_bank(i)[:], lhsT=codes[("k", 0)][:, 0:P].bitcast(FP8X4),
+                                    lhsT_scale=scales[("k", 0)][:, 0:P],
+                                    rhs=codes[("k", 0)][:, 0:512].bitcast(FP8X4), rhs_scale=scales[("k", 0)][:, 0:512],
+                                    start=True, stop=True)
+
+        def whole_turns(i, kk):
+            h = head(i)
+            if kk == 0:
+                whole_t[i] = work.tile([P, 2, 512], I32, name="whole", tag="whole")
+            ts(whole_t[i][:, kk, :], s_ps[(i, kk)][:], TURNS, mul, psit[:, h:h + 1], add)
+
+        def fraction(i, kk):
+            if kk == 0:
+                frac[i] = work.tile([P, 2, 512], F32, name="frac", tag="frac")
+            stt(frac[i][:, kk, :], s_ps[(i, kk)][:], TURNS, mul, whole_t[i][:, kk, :], sub)
+
+        def half_sine(i):
+            h = head(i)
+            x_t[i] = work.tile([P, 1024], F32, name="x", tag="x")
+            sine(x_t[i][:], frac[i][:].rearrange("p a n -> p (a n)"), PI, xb[:, h:h + 1])
+
+        def square_x(i):
+            u_t[i] = work.tile([P, 1024], F32, name="u", tag="u_last" if i == UNITS - 1 else "u", bufs=1)
+            if MODES[i] in "CD":
+                for lo, hi in U_PARTS:
+                    nc.gpsimd.tensor_tensor(out=u_t[i][:, lo:hi], in0=x_t[i][:, lo:hi], in1=x_t[i][:, lo:hi], op=mul)
+            else:
+                nc.scalar.activation(out=u_t[i][:], in_=x_t[i][:], func=ACT.Square)
+
+        def square_term(i):
+            h = head(i)
+            sn = work.tile([P, 1024], F32, name="sn", tag="sn")
+            tb_t[i] = work.tile([P, 1024], F32, name="tb", tag="tb")
+            sine(sn[:], frac[i][:].rearrange("p a n -> p (a n)"), 2 * PI, psir[:, h:h + 1])
+            return lambda: nc.scalar.activation(out=tb_t[i][:], in_=sn[:], func=ACT.Square, scale=al[:, h:h + 1],
+                                                bias=be[:, h:h + 1])
+
+        def cubic_first(i):
+            h = head(i)
+            y_t[i] = work.tile([P, 1024], F32, name="y", tag="y")
+            if MODES[i] in "BC":
+                for lo, hi in (U_PARTS if MODES[i] == "C" else ((0, 1024),)):
+                    nc.scalar.activation(out=y_t[i][:, lo:hi], in_=u_t[i][:, lo:hi], func=ACT.Square, bias=nus[:, h:h + 1])
+            else:
+                stt(y_t[i][:], u_t[i][:], c_a[:, h:h + 1], add, u_t[i][:], mul)
+
+        def cubic_second(i, lo, hi):
+            h = head(i)
+            if lo == 0:
+                ta_t[i] = work.tile([P, 1024], F32, name="ta", tag="ta")
+            if MODES[i] in "BC":
+                stt(ta_t[i][:, lo:hi], u_t[i][:, lo:hi], nk[:, h:h + 1], add, y_t[i][:, lo:hi], mul)
+            else:
+                stt(ta_t[i][:, lo:hi], y_t[i][:, lo:hi], c_b[:, h:h + 1], add, u_t[i][:, lo:hi], mul)
+
+        def turn(i, second, halves=(0, 1)):
+            for kk in halves:
+                if not second:
+                    z_ps[(i, kk)] = psum.tile([P, PACK, P], F32, name="z_ps", tag=("s%d" if i == UNITS - 1 else "z%d") % kk)
+                src = ta_t[i] if second else tb_t[i]
+                for j in range(PACK):
+                    cols = slice(512 * kk + P * j, 512 * kk + P * (j + 1))
+                    nc.tensor.matmul(out=z_ps[(i, kk)][:, j, :], lhsT=src[:, cols], rhs=ident[:],
+                                     start=(not second and j == 0), stop=(second and j == PACK - 1), is_transpose=True)
+
+        def gain(i, kk):
+            h = head(i)
+            if kk == 0:
+                ag_t[i] = work.tile([P, 2, P, PACK], BF16, name="ag", tag="ag", align_bytes=64)
+            const = c_e2 if MODES[i] in "BC" else c_e
+            stt(ag_t[i][:, kk, :, :], z_ps[(i, kk)][:].rearrange("p j n -> p n j"), const[:, h:h + 1], add,
+                gk[:, 2 * h + kk, :, :].to_broadcast([P, P, PACK]), mul)
+
+        def quantize_ag(i, lo, hi):
+            if lo == 0:
+                c = work.tile([P, 2 * P], U32, name="ag_codes", tag="ag_codes", bufs=3, align_bytes=64)
+                s = work.tile([P, 2 * P], U8, name="ag_scales", tag="ag_scales", bufs=3, align_bytes=64)
+                agq[i] = (c, s)
+            c, s = agq[i]
+            nc.vector.quantize_mx(out=c[:, P * lo:P * hi].bitcast(FP8X4), scales=s[:, P * lo:P * hi],
+                                  in_=ag_t[i][:, lo:hi, :, :].rearrange("p a n j -> p (a n j)"))
+
+        def weighted_sum(i, bank, lo, hi, halves=(0, 1)):
+            h = head(i)
+            c, s = agq[i]
+            for kk in halves:
+                acols = slice(P * kk, P * (kk + 1))
+                vcols = slice(512 * kk + lo, 512 * kk + hi)
+                nc.tensor.matmul_mx(out=bank[:, lo:hi], lhsT=c[:, acols].bitcast(FP8X4), lhsT_scale=s[:, acols],
+                                    rhs=codes[("v", h)][:, vcols].bitcast(FP8X4), rhs_scale=scales[("v", h)][:, vcols],
+                                    start=(kk == 0), stop=(kk == 1))
+
+        def result(i, bank, lo, hi):
+            grp, t = divmod(i, PACK)
+            if grp not in o_sb:
+                o_sb[grp] = work.tile([P, PACK, DV], F32, name="o_sb", tag="o_sb")
+            nc.scalar.mul(out=o_sb[grp][:, t, lo:hi], in_=bank[:, lo:hi], mul=1.0 / math.sqrt(TK))
+
+        def store_result(i, count=1):
+            grp, t = divmod(i, PACK)
+            h, gq = divmod(grp, 2)
+            rows = out_0[h, GROUP * gq:GROUP * (gq + 1), :].rearrange("(p t) d -> p t d", t=PACK)
+            nc.sync.dma_start(out=rows[:, t:t + count, :], in_=o_sb[grp][:, t:t + count, :])
+
+        def round_result(grp, lo, hi, eng):
+            if grp not in o_bf:
+                o_bf[grp] = work.tile([P, DV, PACK], BF16, name="o_bf", tag="o_bf", align_bytes=64)
+            src = o_sb[grp][:].rearrange("p t d -> p d t")
+            copy(eng, o_bf[grp][:, lo:hi, :], src[:, lo:hi, :])
+
+        def planes(grp, lo, hi):
+            if grp not in o_q:
+                c = work.tile([P, DV], U32, name="o_codes", tag="o_codes", align_bytes=64)
+                s = work.tile([P, DV], U8, name="o_scales", tag="o_scales", align_bytes=64)
+                o_q[grp] = (c, s)
+            c, s = o_q[grp]
+            nc.vector.quantize_mx(out=c[:, lo:hi].bitcast(FP8X4), scales=s[:, lo:hi],
+                                  in_=o_bf[grp][:, lo:hi, :].rearrange("p d t -> p (d t)"))
+
+        def store_planes(grp, engines):
+            h, gq = divmod(grp, 2)
+            c, s = o_q[grp]
+            cols = slice(DV * h, DV * (h + 1))
+            nc.sync.dma_start(out=out_1[gq, :, cols, :].rearrange("p m t -> p (m t)").bitcast(I32), in_=c[:].bitcast(I32))
+            for quad in range(4):
+                engines[quad].dma_start(out=out_2[gq, 4 * quad:4 * quad + 4, cols].bitcast(I32),
+                                        in_=s[32 * quad:32 * quad + 4, :].bitcast(I32))
+
+        def whole_planes(grp):
+            planes(grp, 0, DV)
+            store_planes(grp, [nc.sync] * 4)
+
+        first = [("k", 0, 0), ("k", 0, 1), ("q", 0, 0), ("k", 0, 2), ("k", 0, 3), ("q", 0, 1)]
+        prep_transpose(first[0])
+        prep_transpose(first[1])
+        prep_transpose(first[2], "o", 2)
+        prep_transpose(first[3], "o", 2)
+        prep_transpose(first[4], "z0", 1)
         absa = small("absa", H, 3)
         absb = small("absb", H, 3)
         m3 = small("m3", H)
@@ -149,15 +341,19 @@ def tile_fourierkolmogorovarnoldattention_x1_kernel(tc, q, k, v, ca, cb, g, out_
         stt(m3[:], absb[:, :, 2], TINY, mx, absa[:, :, 2], add)
         sig = small("sig", H, 1)
         ts(sig[:, :, 0], sig0[:], -1.0, add)
-        nc.vector.reciprocal(out=im3[:], in_=m3[:])
         absab = small("absab", H, 3)
         tt(absab[:], absa[:], absb[:], add)
+        nc.vector.reciprocal(out=im3[:], in_=m3[:])
+        larger = small("larger", H, 3)
+        tt(larger[:], absa[:], absb[:], mx)
+        total = small("total", H)
+        nc.vector.tensor_reduce(out=total[:], in_=absab[:], axis=AX.X, op=add)
         stt(r[:, 0, :], ca_sb[:, :, 2], -1.0, mul, im3[:], mul)
         stt(r[:, 1, :], absb[:, :, 2], TINY, mx, im3[:], mul)
         sine(cs[:], r[:, 0:2, :], PI / 2)
         stt(r[:, 2, :], ca_sb[:, :, 2], -1.0, mul, im3[:], mul)
-        total = small("total", H)
-        nc.vector.tensor_reduce(out=total[:], in_=absab[:], axis=AX.X, op=add)
+        prep_copy(first[0], "A")
+        prep_copy(first[1], "A")
         base = small("base", H)
         ts(base[:], r[:, 0, :], -PI / 6, mul, PI / 6, add)
         ab = small("ab", 2, H, 2)
@@ -166,66 +362,79 @@ def tile_fourierkolmogorovarnoldattention_x1_kernel(tc, q, k, v, ca, cb, g, out_
         nc.vector.tensor_copy(out=ab[:, 1, :, :], in_=cb_sb[:, :, 0:2])
         tt(ba[:, 0, :, :], cb_sb[:, :, 0:2], sig[:].to_broadcast([P, H, 2]), mul)
         stt(ba[:, 1, :, :], ca_sb[:, :, 0:2], -1.0, mul, sig[:].to_broadcast([P, H, 2]), mul)
-        floor = small("floor", H)
-        ts(floor[:], total[:], 2.0 ** -40, mul)
         pr1 = small("pr1", 2, H)
         pr2 = small("pr2", 2, H)
         tt(pr1[:], r[:, 0:2, :], cs[:], mul)
         tt(pr2[:], r[:, 1:3, :], cs[:], mul)
+        floor = small("floor", H)
+        ts(floor[:], total[:], 2.0 ** -40, mul)
         den = small("den", H)
         num = small("num", H)
         tt(den[:], pr1[:, 0, :], pr1[:, 1, :], add)
         tt(num[:], pr2[:, 0, :], pr2[:, 1, :], sub)
+        bound = small("bound", H, 3)
+        stt(bound[:], absab[:], 0.7072, mul, larger[:], add)
         iden = small("iden", H)
         nc.vector.reciprocal(out=iden[:], in_=den[:])
         dm = small("dm", H)
         stt(dm[:], den[:], 32.0, mul, m3[:], mul)
+        c00 = small("c00", H)
+        stt(c00[:], bound[:, :, 0], 0.6, mul, bound[:, :, 1], add)
         z = small("z", H)
         tt(z[:], num[:], iden[:], mul)
+        c0 = small("c0", H)
+        ts(c0[:], c00[:], 0.9205, mul, TINY, mx)
+        ic0 = small("ic0", H)
+        nc.vector.reciprocal(out=ic0[:], in_=c0[:])
+        prep_copy(first[2], "A")
+        prep_quantize(first[0])
         w = small("w", H)
         tt(w[:], z[:], z[:], mul)
         z3 = small("z3", H)
         ts(z3[:], z[:], 1.0 / 3.0, mul)
-        p1 = small("p1", H)
+        pa1 = small("pa1", H)
+        pb1 = small("pb1", H)
+        zw = small("zw", H)
         q1 = small("q1", H)
-        ts(p1[:], w[:], -1.0 / 7.0, mul, 1.0 / 5.0, add)
+        ts(pa1[:], w[:], -1.0 / 3.0, mul, 1.0, add)
+        ts(pb1[:], w[:], -1.0 / 7.0, mul, 1.0 / 5.0, add)
+        tt(zw[:], z3[:], w[:], mul)
         ts(q1[:], w[:], 1.0 / 16.0, mul, -1.0 / 8.0, add)
-        p2 = small("p2", H)
+        pa2 = small("pa2", H)
+        zw2 = small("zw2", H)
         q2 = small("q2", H)
-        tt(p2[:], p1[:], w[:], mul)
+        tt(pa2[:], pa1[:], z3[:], mul)
+        tt(zw2[:], zw[:], w[:], mul)
         tt(q2[:], q1[:], w[:], mul)
-        p3 = small("p3", H)
+        pa3 = small("pa3", H)
+        pb2 = small("pb2", H)
         q3 = small("q3", H)
-        stt(p3[:], p2[:], -1.0 / 3.0, add, w[:], mul)
+        tt(pa3[:], pa2[:], base[:], add)
+        tt(pb2[:], pb1[:], zw2[:], mul)
         stt(q3[:], q2[:], 0.5, add, w[:], mul)
-        e3 = small("e3", H)
-        r32 = small("r32", H)
-        stt(e3[:], p3[:], 1.0, add, z3[:], mul)
-        stt(r32[:], q3[:], 1.0, add, dm[:], mul)
+        prep_quantize(first[1])
         pa = small("pa", H)
-        tt(pa[:], e3[:], base[:], add)
+        tt(pa[:], pa3[:], pb2[:], add)
+        r32 = small("r32", H)
+        stt(r32[:], q3[:], 1.0, add, dm[:], mul)
         cosm = small("cosm", 1, H, 2)
         sinm = small("sinm", 1, H, 2)
         sine(cosm[:, 0, :, 0], pa[:], -1.0, PI / 2)
         sine(cosm[:, 0, :, 1], pa[:], -2.0, PI / 2)
         sine(sinm[:, 0, :, 0], pa[:], 1.0)
         sine(sinm[:, 0, :, 1], pa[:], 2.0)
-        big_k = small("big_k", H, 1)
-        tt(big_k[:, :, 0], r32[:], floor[:], mx)
+        prep_copy(first[3], "A")
+        prep_copy(first[4], "A")
+        prep_quantize(first[2])
+        scores(0, 0)
         phi = small("phi", H)
         tt(phi[:], pa[:], sig[:, :, 0], mul)
-        ik = small("ik", H, 1)
-        nc.vector.reciprocal(out=ik[:, :, 0], in_=big_k[:, :, 0])
+        big_k = small("big_k", H, 1)
+        tt(big_k[:, :, 0], r32[:], floor[:], mx)
         phit = small("phit", H)
         ts(phit[:], phi[:], 1.0 / (2 * PI), mul)
-        xb = small("xb", H)
-        ts(xb[:], phi[:], -0.5, mul)
-
-        prologue = [("k", 0, 0), ("k", 0, 1), ("q", 0, 0), ("k", 0, 2), ("k", 0, 3), ("q", 0, 1)]
-        prep_transpose(prologue[0])
-        prep_copy(prologue[0])
-        prep_transpose(prologue[1])
-
+        ik = small("ik", H, 1)
+        nc.vector.reciprocal(out=ik[:, :, 0], in_=big_k[:, :, 0])
         rc = small("rc", 2, H * 2)
         rs = small("rs", 2, H * 2)
         tt(rc[:], ab[:].rearrange("p a h m -> p a (h m)"),
@@ -234,28 +443,26 @@ def tile_fourierkolmogorovarnoldattention_x1_kernel(tc, q, k, v, ca, cb, g, out_
            sinm[:].rearrange("p a h m -> p a (h m)").to_broadcast([P, 2, H * 2]), mul)
         rot = small("rot", 2, H, 2)
         tt(rot[:].rearrange("p a h m -> p a (h m)"), rc[:], rs[:], add)
-        absr = small("absr", H, 2)
-        stt(absr[:], rot[:, 1, :, :], -1.0, mul, rot[:, 1, :, :], mx)
+        prep_quantize(first[3])
+        rho = small("rho", H)
+        tt(rho[:], rot[:, 1, :, 1], ic0[:], mul)
+        ts(xb[:], phi[:], -0.5, mul)
         ak = small("ak", H, 2)
         tt(ak[:], rot[:, 0, :, :], ik[:].to_broadcast([P, H, 2]), mul)
-        mm = small("mm", H)
-        stt(mm[:], absr[:, :, 1], TINY, mx, absr[:, :, 0], add)
         nm = small("nm", 2, H)
         tt(nm[:, 1, :], rot[:, 1, :, 0], ik[:, :, 0], mul)
-        imm = small("imm", H)
-        nc.vector.reciprocal(out=imm[:], in_=mm[:])
-        mk = small("mk", H)
-        stt(mk[:], mm[:], 2.0, mul, ik[:, :, 0], mul)
-        rho = small("rho", H)
-        ar = small("ar", H)
-        tt(rho[:], rot[:, 1, :, 1], imm[:], mul)
-        tt(ar[:], absr[:, :, 1], imm[:], mul)
-        psit = small("psit", H)
         stt(psit[:], rho[:], 1.0 / 8.0, mul, phit[:], sub)
+        ar = small("ar", H)
+        stt(ar[:], rho[:], -1.0, mul, rho[:], mx)
+        stt(psir[:], rho[:], PI / 4, mul, phi[:], sub)
+        mk = small("mk", H)
+        stt(mk[:], c0[:], 2.0, mul, ik[:, :, 0], mul)
         zr = small("zr", H)
         ts(zr[:], ar[:], 1e-4, mx)
-        psir = small("psir", H)
-        stt(psir[:], rho[:], PI / 4, mul, phi[:], sub)
+        prep_quantize(first[4])
+        whole_turns(0, 0)
+        scores(0, 1)
+        prep_transpose(first[5], "z1", 1)
         dn = small("dn", 2, H)
         sd = small("sd", H)
         c2d = small("c2d", H)
@@ -263,223 +470,218 @@ def tile_fourierkolmogorovarnoldattention_x1_kernel(tc, q, k, v, ca, cb, g, out_
         sine(sd[:], rho[:], PI / 4)
         sine(c2d[:], ar[:], -PI / 2, PI / 2)
         sine(dn[:, 0, :], zr[:], PI / 2)
-        tt(nm[:, 0, :], mk[:], zr[:], mul)
-
-        prep_copy(prologue[1])
-        prep_quantize(prologue[0])
-        prep_transpose(prologue[2])
-        prep_copy(prologue[2])
-        prep_transpose(prologue[3])
 
         idn = small("idn", 2, H)
-        nc.vector.reciprocal(out=idn[:], in_=dn[:])
-        prep_quantize(prologue[1])
         ml = small("ml", 2, H)
-        tt(ml[:], nm[:], idn[:], mul)
-        al = small("al", H)
-        nc.gpsimd.tensor_tensor(out=al[:], in0=ml[:, 0, :], in1=half_t[:], op=ALU.pow)
-        gk = small("gk", H * 2, 1, PACK)
-        tt(gk[:].rearrange("p (h kk) o j -> p h (kk o j)", h=H), g_sb[:].rearrange("p (h kk) j -> p h (kk j)", h=H),
-           big_k[:].to_broadcast([P, H, 2 * PACK]), mul)
         t_a2 = small("t_a2", H)
         t_a1 = small("t_a1", H)
-        stt(t_a2[:], ml[:, 0, :], 0.5, mul, c2d[:], mul)
-        tt(t_a1[:], ml[:, 1, :], sd[:], mul)
         a2 = small("a2", H)
         a1 = small("a1", H)
-        tt(a2[:], t_a2[:], ak[:, :, 1], add)
-        tt(a1[:], ak[:, :, 0], t_a1[:], sub)
-
-        prep_copy(prologue[3])
-        prep_quantize(prologue[2])
-        prep_transpose(prologue[4])
-        prep_copy(prologue[4])
-        prep_transpose(prologue[5])
-
-        c_a = small("c_a", H)
-        ts(c_a[:], a2[:], 8.0, mul, -1.5, add)
-        b0 = small("b0", H)
-        stt(b0[:], a2[:], 4.0, mul, a1[:], add)
         e0 = small("e0", H)
-        stt(e0[:], a2[:], -1.0 / 32.0, add, a1[:], add)
         ial = small("ial", H)
-        nc.vector.reciprocal(out=ial[:], in_=al[:])
-        c_b = small("c_b", H)
-        ts(c_b[:], b0[:], -2.0, mul, 9.0 / 16.0, add)
-        be = small("be", H)
-        stt(be[:], ml[:, 1, :], 0.5, mul, ial[:], mul)
         e1 = small("e1", H)
-        stt(e1[:], ml[:, 0, :], -0.5, mul, e0[:], add)
         be2 = small("be2", H)
-        tt(be2[:], be[:], be[:], mul)
-        prep_quantize(prologue[3])
-        c_e = small("c_e", H)
-        tt(c_e[:], e1[:], be2[:], sub)
-        prep_quantize(prologue[4])
-        prep_copy(prologue[5])
+        wq = small("wq", H)
+        sq16 = small("sq16", H)
+        disc = small("disc", H)
+        root = small("root", H)
+        dd = small("dd", H)
+        idd = small("idd", H)
+        nus0 = small("nus0", H)
+        us2 = small("us2", H)
+        e3 = small("e3", H)
+        b0 = small("b0", H)
+        late = [
+            [lambda: tt(nm[:, 0, :], mk[:], zr[:], mul), lambda: nc.vector.reciprocal(out=idn[:], in_=dn[:])],
+            [lambda: tt(ml[:], nm[:], idn[:], mul),
+             lambda: nc.gpsimd.tensor_tensor(out=al[:], in0=ml[:, 0, :], in1=half_t[:], op=ALU.pow)],
+            [lambda: stt(t_a2[:], ml[:, 0, :], 0.5, mul, c2d[:], mul), lambda: tt(t_a1[:], ml[:, 1, :], sd[:], mul)],
+            [lambda: tt(a2[:], t_a2[:], ak[:, :, 1], add), lambda: tt(a1[:], ak[:, :, 0], t_a1[:], sub),
+             lambda: nc.vector.reciprocal(out=ial[:], in_=al[:])],
+            [lambda: ts(wq[:], a1[:], 3.0 / 32.0, add), lambda: stt(sq16[:], a2[:], 16.0, mul, a2[:], mul),
+             lambda: stt(be[:], ml[:, 1, :], 0.5, mul, ial[:], mul), lambda: ts(c_a[:], a2[:], 8.0, mul, -1.5, add),
+             lambda: stt(b0[:], a2[:], 4.0, mul, a1[:], add)],
+            [lambda: stt(disc[:], wq[:], 1.5, mul, sq16[:], add),
+             lambda: nc.gpsimd.tensor_tensor(out=root[:], in0=disc[:], in1=half_t[:], op=ALU.pow),
+             lambda: stt(e0[:], a2[:], -1.0 / 32.0, add, a1[:], add), lambda: tt(be2[:], be[:], be[:], mul),
+             lambda: ts(c_b[:], b0[:], -2.0, mul, 9.0 / 16.0, add)],
+            [lambda: stt(e1[:], ml[:, 0, :], -0.5, mul, e0[:], add),
+             lambda: tt(gk[:].rearrange("p (h kk) o j -> p h (kk o j)", h=H),
+                        g_sb[:].rearrange("p (h kk) j -> p h (kk j)", h=H), big_k[:].to_broadcast([P, H, 2 * PACK]), mul),
+             lambda: stt(dd[:], a2[:], 4.0, mul, root[:], add)],
+            [lambda: tt(c_e[:], e1[:], be2[:], sub), lambda: nc.vector.reciprocal(out=idd[:], in_=dd[:])],
+            [lambda: stt(nus0[:], wq[:], -1.0, mul, idd[:], mul)],
+            [lambda: ts(nus[:], nus0[:], -0.5, add)],
+            [lambda: stt(nk[:], nus[:], -2.0, mul, c_a[:], add), lambda: tt(us2[:], nus[:], nus[:], mul)],
+            [lambda: tt(e3[:], nk[:], us2[:], mul)],
+            [lambda: tt(c_e2[:], c_e[:], e3[:], sub)],
+        ]
 
-        s_ps, frac, u_t, tb_t, t2_t, ta_t, z_ps, ag_t, agq, o_ps, o_sb, o_bf = ({} for n in range(12))
-
-        def head(i):
-            return i // 8
-
-        def scores(i):
-            h = head(i)
-            qcols = slice(P * (i % 8), P * (i % 8 + 1))
-            for kk in range(2):
-                bank = psum.tile([P, 512], F32, name="s_ps", tag="s%d" % kk)
-                kcols = slice(512 * kk, 512 * (kk + 1))
-                nc.tensor.matmul_mx(out=bank[:], lhsT=codes[("q", h)][:, qcols].bitcast(FP8X4),
-                                    lhsT_scale=scales[("q", h)][:, qcols],
-                                    rhs=codes[("k", h)][:, kcols].bitcast(FP8X4), rhs_scale=scales[("k", h)][:, kcols],
-                                    start=True, stop=True)
-                s_ps[(i, kk)] = bank
-
-        def reduce_angle(i):
-            h = head(i)
-            whole = work.tile([P, 2, 512], I32, name="whole", tag="whole")
-            f = work.tile([P, 2, 512], F32, name="frac", tag="frac")
-            for kk in range(2):
-                ts(whole[:, kk, :], s_ps[(i, kk)][:], TURNS, mul, psit[:, h:h + 1], add)
-            for kk in range(2):
-                stt(f[:, kk, :], s_ps[(i, kk)][:], TURNS, mul, whole[:, kk, :], sub)
-            frac[i] = f
-
-        def sines(i):
-            h = head(i)
-            f = frac[i][:].rearrange("p a n -> p (a n)")
-            x = work.tile([P, 1024], F32, name="x", tag="x")
-            sn = work.tile([P, 1024], F32, name="sn", tag="sn")
-            u = work.tile([P, 1024], F32, name="u", tag="u")
-            tb = work.tile([P, 1024], F32, name="tb", tag="tb")
-            sine(x[:], f, PI, xb[:, h:h + 1])
-            sine(sn[:], f, 2 * PI, psir[:, h:h + 1])
-            nc.scalar.activation(out=u[:], in_=x[:], func=ACT.Square)
-            nc.scalar.activation(out=tb[:], in_=sn[:], func=ACT.Square, scale=al[:, h:h + 1], bias=be[:, h:h + 1])
-            u_t[i], tb_t[i] = u, tb
-
-        def cubic_first(i):
-            h = head(i)
-            t2 = work.tile([P, 1024], F32, name="t2", tag="t2")
-            stt(t2[:], u_t[i][:], c_a[:, h:h + 1], add, u_t[i][:], mul)
-            t2_t[i] = t2
-
-        def cubic_second(i):
-            h = head(i)
-            ta = work.tile([P, 1024], F32, name="ta", tag="ta")
-            stt(ta[:], t2_t[i][:], c_b[:, h:h + 1], add, u_t[i][:], mul)
-            ta_t[i] = ta
-
-        def turn_and_add(i):
-            for kk in range(2):
-                bank = psum.tile([P, PACK, P], F32, name="z_ps", tag="z%d" % kk)
-                for j in range(PACK):
-                    cols = slice(512 * kk + P * j, 512 * kk + P * (j + 1))
-                    nc.tensor.matmul(out=bank[:, j, :], lhsT=tb_t[i][:, cols], rhs=ident[:], start=True, stop=False,
-                                     is_transpose=True)
-                    nc.tensor.matmul(out=bank[:, j, :], lhsT=ta_t[i][:, cols], rhs=ident[:], start=False, stop=True,
-                                     is_transpose=True)
-                z_ps[(i, kk)] = bank
-
-        def gain(i):
-            h = head(i)
-            ag = work.tile([P, 2, P, PACK], BF16, name="ag", tag="ag", align_bytes=64)
-            for kk in range(2):
-                stt(ag[:, kk, :, :], z_ps[(i, kk)][:].rearrange("p j n -> p n j"), c_e[:, h:h + 1], add,
-                    gk[:, 2 * h + kk, :, :].to_broadcast([P, P, PACK]), mul)
-            ag_t[i] = ag
-
-        def quantize_ag(i):
-            c = work.tile([P, 2 * P], U32, name="ag_codes", tag="ag_codes", align_bytes=64)
-            s = work.tile([P, 2 * P], U8, name="ag_scales", tag="ag_scales", align_bytes=64)
-            nc.vector.quantize_mx(out=c[:].bitcast(FP8X4), scales=s[:], in_=ag_t[i][:].rearrange("p a n j -> p (a n j)"))
-            agq[i] = (c, s)
-
-        def weighted_sum(i):
-            h = head(i)
-            c, s = agq[i]
-            bank = psum.tile([P, DV], F32, name="o_ps", tag="o", bufs=2)
-            for kk in range(2):
-                acols = slice(P * kk, P * (kk + 1))
-                vcols = slice(512 * kk, 512 * (kk + 1))
-                nc.tensor.matmul_mx(out=bank[:], lhsT=c[:, acols].bitcast(FP8X4), lhsT_scale=s[:, acols],
-                                    rhs=codes[("v", h)][:, vcols].bitcast(FP8X4), rhs_scale=scales[("v", h)][:, vcols],
-                                    start=(kk == 0), stop=(kk == 1))
-            o_ps[i] = bank
-
-        def result(i):
-            grp, t = divmod(i, PACK)
-            h, gq = divmod(grp, 2)
-            if t == 0:
-                o_sb[grp] = work.tile([P, PACK, DV], F32, name="o_sb", tag="o_sb")
-            nc.scalar.mul(out=o_sb[grp][:, t, :], in_=o_ps[i][:], mul=1.0 / math.sqrt(TK))
-            rows = out_0[h, GROUP * gq:GROUP * (gq + 1), :].rearrange("(p t) d -> p t d", t=PACK)
-            nc.sync.dma_start(out=rows[:, t, :], in_=o_sb[grp][:, t, :])
-
-        def round_result(grp, split):
-            o_bf[grp] = work.tile([P, DV, PACK], BF16, name="o_bf", tag="o_bf", align_bytes=64)
-            src = o_sb[grp][:].rearrange("p t d -> p d t")
-            if split > 0:
-                nc.vector.tensor_copy(out=o_bf[grp][:, 0:split, :], in_=src[:, 0:split, :])
-            if split < DV:
-                nc.scalar.copy(out=o_bf[grp][:, split:DV, :], in_=src[:, split:DV, :])
-
-        def planes(grp):
-            h, gq = divmod(grp, 2)
-            c = work.tile([P, DV], U32, name="o_codes", tag="o_codes", align_bytes=64)
-            s = work.tile([P, DV], U8, name="o_scales", tag="o_scales", align_bytes=64)
-            nc.vector.quantize_mx(out=c[:].bitcast(FP8X4), scales=s[:], in_=o_bf[grp][:].rearrange("p d t -> p (d t)"))
-            cols = slice(DV * h, DV * (h + 1))
-            nc.sync.dma_start(out=out_1[gq, :, cols, :].rearrange("p m t -> p (m t)").bitcast(I32), in_=c[:].bitcast(I32))
-            for quad in range(4):
-                nc.sync.dma_start(out=out_2[gq, 4 * quad:4 * quad + 4, cols].bitcast(I32),
-                                  in_=s[32 * quad:32 * quad + 4, :].bitcast(I32))
+        def constants(n):
+            for call in late[n]:
+                call()
 
         jobs = {-2: ("q", 0, 2), -1: ("q", 0, 3), 0: ("k", 1, 0), 1: ("k", 1, 1), 2: ("k", 1, 2), 3: ("k", 1, 3),
-                4: ("q", 1, 0), 5: ("q", 1, 1), 6: ("q", 1, 2), 7: ("q", 1, 3), -3: prologue[5]}
+                4: ("q", 1, 0), 5: ("q", 1, 1), 6: ("q", 1, 2), 7: ("q", 1, 3)}
+        extras = {(i, e): [] for i in range(UNITS + 1) for e in "AVPL"}
+        for n in range(4):
+            step, eng = V0_PLAN[n]
+            extras[(step, eng)].append(lambda n=n, eng=eng: v_interleave(0, 1, n, eng))
+        extras[(V0_PLAN[4], "V")].append(lambda: v_quantize(0, 1))
+        for n in range(8):
+            step, eng = V1_PLAN[n]
+            extras[(step, eng)].append(lambda n=n, eng=eng: v_interleave(1, n // 4, n % 4, eng))
+        extras[(V1_PLAN[8], "V")].append(lambda: v_quantize(1, 0))
+        extras[(V1_PLAN[9], "V")].append(lambda: v_quantize(1, 1))
+        for grp in range(3):
+            for n in range(4):
+                step, eng = CAST_PLAN[grp][n]
+                extras[(step, eng)].append(lambda grp=grp, n=n, eng=eng: round_result(grp, n * P, (n + 1) * P, eng))
+            extras[(CAST_PLAN[grp][4], "V")].append(lambda grp=grp: whole_planes(grp))
+
+        def extra(i, eng):
+            for call in extras[(i, eng)]:
+                call()
 
         def live(i):
             return 0 <= i < UNITS
 
-        scores(0)
-        for i in range(-2, UNITS + 2):
-            if live(i + 1):
-                sines(i + 1)
-            if live(i):
-                cubic_first(i)
-            if live(i - 1):
-                quantize_ag(i - 1)
-                weighted_sum(i - 1)
-            if i - 1 in jobs:
+        def finish_unit(i):
+            weighted_sum(i, out_bank(i), 0, DV)
+            result(i, o_ps[i], 0, DV)
+            store_result(i)
+
+        for n in range(V0_HEAD):
+            v_interleave(0, 0, n, "A")
+        prep_copy(first[5], "A")
+        constants(0)
+        whole_turns(0, 1)
+        constants(1)
+        fraction(0, 0)
+        scores(1, 0)
+        constants(2)
+        fraction(0, 1)
+        scores(1, 1)
+        prep_transpose(jobs[-2])
+        prep_transpose(jobs[-1])
+        half_sine(0)
+        square_x(0)
+        finish = square_term(0)
+        constants(3)
+        prep_quantize(first[5])
+        constants(4)
+        finish()
+        whole_turns(1, 0)
+        constants(5)
+        whole_turns(1, 1)
+        constants(6)
+        fraction(1, 0)
+        constants(7)
+        fraction(1, 1)
+        scores(2, 0)
+        scores(2, 1)
+        half_sine(1)
+        constants(8)
+        cubic_first(0)
+        constants(9)
+        turn(0, False)
+        prep_copy(jobs[-2], FILL_ON[0])
+        constants(10)
+        for n in range(V0_HEAD, 4):
+            v_interleave(0, 0, n, FILL_ON[2])
+        constants(11)
+        prep_copy(jobs[-1], FILL_ON[1])
+        constants(12)
+        extras[(1, "V")].append(lambda: prep_quantize(jobs[-2]))
+        extras[(1, "V")].append(lambda: v_quantize(0, 0))
+
+        last = UNITS - 1
+        for i in range(last - 1):
+            finish = square_term(i + 1)
+            if i - 1 in jobs and i > 0:
                 prep_quantize(jobs[i - 1])
-            if live(i):
-                cubic_second(i)
-                turn_and_add(i)
-            if live(i + 2):
-                reduce_angle(i + 2)
+            if i == 2:
+                prep_quantize(jobs[-1])
+            extra(i, "V")
+            if i > 0 and MODES[i] in "AD":
+                cubic_first(i)
+            if i > 0:
+                quantize_ag(i - 1, 0, 2)
+            if i == AV_START:
+                for n in range(AV_START - 1):
+                    finish_unit(n)
+            if i >= AV_START:
+                weighted_sum(i - 1, out_bank(i - 1), 0, DV)
             if i in jobs:
                 prep_transpose(jobs[i])
+            if i >= AV_START:
+                keep_warm(i, WARM[0])
+                result(i - 1, o_ps[i - 1], 0, DV)
+                store_result(i - 1)
+            cubic_second(i, 0, 1024)
+            turn(i, True)
+            if i >= AV_START:
+                keep_warm(i, WARM[1])
+            if i in jobs and PREP_ON[i] == "A":
+                prep_copy(jobs[i], "A")
+            extra(i, "A")
+            square_x(i + 1)
+            extra(i, "P")
+            finish()
+            extra(i, "L")
+            whole_turns(i + 2, 0)
+            whole_turns(i + 2, 1)
+            fraction(i + 2, 0)
+            fraction(i + 2, 1)
+            if i in jobs and PREP_ON[i] == "V":
+                prep_copy(jobs[i], "V")
             if live(i + 3):
-                scores(i + 3)
-            if i == -2:
-                v_interleave(0, 0, True)
-            if i == -1:
-                v_quantize(0, 0)
-                v_interleave(0, 1, True)
-            if i == 0:
-                v_quantize(0, 1)
-            if i in (7, 8):
-                v_quantize(1, i - 7)
-            if i >= 2 and (i - 2) % PACK == 0 and i > 2:
-                planes((i - 2) // PACK - 1)
-            if live(i - 1):
-                result(i - 1)
-            if i in jobs:
-                prep_copy(jobs[i])
-            if i in (6, 7):
-                v_interleave(1, i - 6, False)
-            if live(i):
-                gain(i)
-            if i >= PACK and i % PACK == 0:
-                round_result(i // PACK - 1, 1280 // PACK if i == UNITS else 0)
-        planes(3)
+                scores(i + 3, 0)
+                scores(i + 3, 1)
+            if MODES[i + 1] in "BC":
+                cubic_first(i + 1)
+            half_sine(i + 2)
+            gain(i, 0)
+            gain(i, 1)
+            turn(i + 1, False)
+
+        square_x(last)
+        square_term(last)()
+        if MODES[last - 1] in "AD":
+            cubic_first(last - 1)
+        quantize_ag(last - 2, 0, 2)
+        finish_unit(last - 2)
+        extra(last - 1, "A")
+        cubic_second(last - 1, 0, 1024)
+        turn(last - 1, True)
+        cubic_first(last)
+        turn(last, False)
+        gain(last - 1, 0)
+        gain(last - 1, 1)
+        cubic_second(last, 0, 512)
+        turn(last, True, (0,))
+        quantize_ag(last - 1, 0, 2)
+        cubic_second(last, 512, 1024)
+        weighted_sum(last - 1, out_bank(last - 1), 0, DV)
+        turn(last, True, (1,))
+        result(last - 1, o_ps[last - 1], 0, DV)
+        extra(last - 1, "V")
+        gain(last, 0)
+        gain(last, 1)
+        other = psum.tile([P, DV], F32, name="o_ps", tag="z0")
+        quantize_ag(last, 0, 1)
+        weighted_sum(last, out_bank(last), 0, 256, (0,))
+        weighted_sum(last, other, 256, DV, (0,))
+        quantize_ag(last, 1, 2)
+        weighted_sum(last, out_bank(last), 0, 256, (1,))
+        weighted_sum(last, other, 256, DV, (1,))
+        extra(last, "V")
+        result(last, o_ps[last], 0, 256)
+        round_result(3, 0, 256, "V")
+        result(last, other, 256, DV)
+        store_result(last - 1, 2)
+        round_result(3, 256, 384, "A")
+        round_result(3, 384, DV, "V")
+        planes(3, 0, 256)
+        planes(3, 256, DV)
+        store_planes(3, [nc.scalar, nc.scalar, nc.sync, nc.sync])

@@ -26,14 +26,17 @@ TURNS = 1.0 / (2.0 * PI * math.sqrt(E))
 TINY = 1e-37
 MODES = "ACCCCCCCCCCCCCDA"
 U_PARTS = ((0, 1024),)
-WARM = (0, 0)
+WARM = (0, 0, 0, 0, 0)
+AV_EARLY = 0
 AV_START = 2
 V0_HEAD = 4
-FILL_ON = "VAA"
-PREP_ON = "AAAAAAAA"
-V0_PLAN = ((0, "L"), (0, "L"), (1, "L"), (1, "V"), 2)
-V1_PLAN = ((2, "V"), (3, "V"), (3, "V"), (4, "V"), (4, "V"), (5, "V"), (5, "V"), (6, "V"), 7, 8)
-CAST_PLAN = (((7, "V"), (8, "V"), (8, "L"), (9, "V"), 10), ((9, "L"), (10, "L"), (11, "V"), (11, "V"), 12), ((12, "L"), (13, "V"), (13, "L"), (13, "V"), 14))
+V00_AT = 1
+V00_PLAN = ((0, "V"), (0, "V"), (0, "V"), (0, "V"))
+FILL_ON = "AAV"
+PREP_ON = "AAVAVAVA"
+V0_PLAN = ((0, "V"), (0, "P"), (1, "L"), (1, "P"), 2)
+V1_PLAN = ((2, "P"), (2, "P"), (3, "P"), (4, "P"), (4, "P"), (5, "P"), (6, "P"), (6, "P"), 5, 7)
+CAST_PLAN = (((7, "P"), (8, "P"), (9, "P"), (10, "P"), 11), ((9, "V"), (10, "V"), (11, "P"), (11, "L"), 12), ((12, "P"), (13, "P"), (13, "V"), (13, "L"), 14))
 
 
 def tile_fourierkolmogorovarnoldattention_x1_kernel(tc, q, k, v, ca, cb, g, out_0, out_1, out_2):
@@ -120,7 +123,7 @@ def tile_fourierkolmogorovarnoldattention_x1_kernel(tc, q, k, v, ca, cb, g, out_
                                   in_=grouped[job][:])
 
         def v_interleave(h, kk, part, eng):
-            if part == 0:
+            if ("v", h, kk) not in grouped:
                 grouped[("v", h, kk)] = work.tile([P, 512, PACK], BF16, name="vgrouped", tag="vgrouped", align_bytes=64)
             cols = slice(128 * part, 128 * (part + 1))
             copy(eng, grouped[("v", h, kk)][:, cols, :], raw[("v", h, kk)][:].rearrange("p j d -> p d j")[:, cols, :])
@@ -186,9 +189,10 @@ def tile_fourierkolmogorovarnoldattention_x1_kernel(tc, q, k, v, ca, cb, g, out_
                 o_ps[i] = psum.tile([P, DV], F32, name="o_ps", tag="o", bufs=2)
             return o_ps[i]
 
-        def keep_warm(i, n):
+        def keep_warm(n):
             for rep in range(n):
-                nc.tensor.matmul_mx(out=out_bank(i)[:], lhsT=codes[("k", 0)][:, 0:P].bitcast(FP8X4),
+                spare = psum.tile([P, 512], F32, name="spare", tag="xt", bufs=2)
+                nc.tensor.matmul_mx(out=spare[:], lhsT=codes[("k", 0)][:, 0:P].bitcast(FP8X4),
                                     lhsT_scale=scales[("k", 0)][:, 0:P],
                                     rhs=codes[("k", 0)][:, 0:512].bitcast(FP8X4), rhs_scale=scales[("k", 0)][:, 0:512],
                                     start=True, stop=True)
@@ -263,8 +267,8 @@ def tile_fourierkolmogorovarnoldattention_x1_kernel(tc, q, k, v, ca, cb, g, out_
 
         def quantize_ag(i, lo, hi):
             if lo == 0:
-                c = work.tile([P, 2 * P], U32, name="ag_codes", tag="ag_codes", bufs=3, align_bytes=64)
-                s = work.tile([P, 2 * P], U8, name="ag_scales", tag="ag_scales", bufs=3, align_bytes=64)
+                c = work.tile([P, 2 * P], U32, name="ag_codes", tag="ag_codes", bufs=AV_START + 1, align_bytes=64)
+                s = work.tile([P, 2 * P], U8, name="ag_scales", tag="ag_scales", bufs=AV_START + 1, align_bytes=64)
                 agq[i] = (c, s)
             c, s = agq[i]
             nc.vector.quantize_mx(out=c[:, P * lo:P * hi].bitcast(FP8X4), scales=s[:, P * lo:P * hi],
@@ -283,7 +287,7 @@ def tile_fourierkolmogorovarnoldattention_x1_kernel(tc, q, k, v, ca, cb, g, out_
         def result(i, bank, lo, hi):
             grp, t = divmod(i, PACK)
             if grp not in o_sb:
-                o_sb[grp] = work.tile([P, PACK, DV], F32, name="o_sb", tag="o_sb")
+                o_sb[grp] = work.tile([P, PACK, DV], F32, name="o_sb", tag="o_sb", bufs=3)
             nc.scalar.mul(out=o_sb[grp][:, t, lo:hi], in_=bank[:, lo:hi], mul=1.0 / math.sqrt(TK))
 
         def store_result(i, count=1):
@@ -455,14 +459,14 @@ def tile_fourierkolmogorovarnoldattention_x1_kernel(tc, q, k, v, ca, cb, g, out_
         ar = small("ar", H)
         stt(ar[:], rho[:], -1.0, mul, rho[:], mx)
         stt(psir[:], rho[:], PI / 4, mul, phi[:], sub)
-        mk = small("mk", H)
-        stt(mk[:], c0[:], 2.0, mul, ik[:, :, 0], mul)
+        prep_quantize(first[4])
         zr = small("zr", H)
         ts(zr[:], ar[:], 1e-4, mx)
-        prep_quantize(first[4])
         whole_turns(0, 0)
         scores(0, 1)
         prep_transpose(first[5], "z1", 1)
+        mk = small("mk", H)
+        stt(mk[:], c0[:], 2.0, mul, ik[:, :, 0], mul)
         dn = small("dn", 2, H)
         sd = small("sd", H)
         c2d = small("c2d", H)
@@ -527,6 +531,9 @@ def tile_fourierkolmogorovarnoldattention_x1_kernel(tc, q, k, v, ca, cb, g, out_
         for n in range(4):
             step, eng = V0_PLAN[n]
             extras[(step, eng)].append(lambda n=n, eng=eng: v_interleave(0, 1, n, eng))
+        for n in range(V0_HEAD, 4):
+            step, eng = V00_PLAN[n]
+            extras[(step, eng)].append(lambda n=n, eng=eng: v_interleave(0, 0, n, eng))
         extras[(V0_PLAN[4], "V")].append(lambda: v_quantize(0, 1))
         for n in range(8):
             step, eng = V1_PLAN[n]
@@ -553,20 +560,20 @@ def tile_fourierkolmogorovarnoldattention_x1_kernel(tc, q, k, v, ca, cb, g, out_
 
         for n in range(V0_HEAD):
             v_interleave(0, 0, n, "A")
-        prep_copy(first[5], "A")
         constants(0)
-        whole_turns(0, 1)
-        constants(1)
         fraction(0, 0)
         scores(1, 0)
+        constants(1)
+        whole_turns(0, 1)
         constants(2)
+        prep_copy(first[5], FILL_ON[2])
         fraction(0, 1)
         scores(1, 1)
         prep_transpose(jobs[-2])
         prep_transpose(jobs[-1])
         half_sine(0)
-        square_x(0)
         finish = square_term(0)
+        square_x(0)
         constants(3)
         prep_quantize(first[5])
         constants(4)
@@ -586,18 +593,15 @@ def tile_fourierkolmogorovarnoldattention_x1_kernel(tc, q, k, v, ca, cb, g, out_
         constants(9)
         turn(0, False)
         prep_copy(jobs[-2], FILL_ON[0])
-        constants(10)
-        for n in range(V0_HEAD, 4):
-            v_interleave(0, 0, n, FILL_ON[2])
-        constants(11)
         prep_copy(jobs[-1], FILL_ON[1])
-        constants(12)
         extras[(1, "V")].append(lambda: prep_quantize(jobs[-2]))
-        extras[(1, "V")].append(lambda: v_quantize(0, 0))
+        extras[(V00_AT, "V")].append(lambda: v_quantize(0, 0))
 
         last = UNITS - 1
         for i in range(last - 1):
             finish = square_term(i + 1)
+            if i == 1:
+                constants(10)
             if i - 1 in jobs and i > 0:
                 prep_quantize(jobs[i - 1])
             if i == 2:
@@ -605,8 +609,12 @@ def tile_fourierkolmogorovarnoldattention_x1_kernel(tc, q, k, v, ca, cb, g, out_
             extra(i, "V")
             if i > 0 and MODES[i] in "AD":
                 cubic_first(i)
+            if i == 1:
+                constants(11)
             if i > 0:
                 quantize_ag(i - 1, 0, 2)
+            if i == 1:
+                constants(12)
             if i == AV_START:
                 for n in range(AV_START - 1):
                     finish_unit(n)
@@ -615,13 +623,12 @@ def tile_fourierkolmogorovarnoldattention_x1_kernel(tc, q, k, v, ca, cb, g, out_
             if i in jobs:
                 prep_transpose(jobs[i])
             if i >= AV_START:
-                keep_warm(i, WARM[0])
                 result(i - 1, o_ps[i - 1], 0, DV)
                 store_result(i - 1)
             cubic_second(i, 0, 1024)
             turn(i, True)
-            if i >= AV_START:
-                keep_warm(i, WARM[1])
+            if i > 8:
+                keep_warm(WARM[0])
             if i in jobs and PREP_ON[i] == "A":
                 prep_copy(jobs[i], "A")
             extra(i, "A")
@@ -638,6 +645,8 @@ def tile_fourierkolmogorovarnoldattention_x1_kernel(tc, q, k, v, ca, cb, g, out_
             if live(i + 3):
                 scores(i + 3, 0)
                 scores(i + 3, 1)
+            else:
+                keep_warm(WARM[1])
             if MODES[i + 1] in "BC":
                 cubic_first(i + 1)
             half_sine(i + 2)
@@ -645,6 +654,7 @@ def tile_fourierkolmogorovarnoldattention_x1_kernel(tc, q, k, v, ca, cb, g, out_
             gain(i, 1)
             turn(i + 1, False)
 
+        keep_warm(WARM[2])
         square_x(last)
         square_term(last)()
         if MODES[last - 1] in "AD":
@@ -654,16 +664,21 @@ def tile_fourierkolmogorovarnoldattention_x1_kernel(tc, q, k, v, ca, cb, g, out_
         extra(last - 1, "A")
         cubic_second(last - 1, 0, 1024)
         turn(last - 1, True)
+        keep_warm(WARM[3])
         cubic_first(last)
         turn(last, False)
+        keep_warm(WARM[4])
         gain(last - 1, 0)
         gain(last - 1, 1)
         cubic_second(last, 0, 512)
         turn(last, True, (0,))
         quantize_ag(last - 1, 0, 2)
         cubic_second(last, 512, 1024)
-        weighted_sum(last - 1, out_bank(last - 1), 0, DV)
+        if AV_EARLY:
+            weighted_sum(last - 1, out_bank(last - 1), 0, DV)
         turn(last, True, (1,))
+        if not AV_EARLY:
+            weighted_sum(last - 1, out_bank(last - 1), 0, DV)
         result(last - 1, o_ps[last - 1], 0, DV)
         extra(last - 1, "V")
         gain(last, 0)

@@ -28,15 +28,17 @@ MODES = "ACCCCCCCCCCCCCDA"
 U_PARTS = ((0, 1024),)
 WARM = (0, 0, 0, 0, 0)
 AV_EARLY = 0
+Y_PARTS = ((0, 512), (512, 1024))
+EVAC_ON = "AAAVAAAAAVAAAAAA"
 AV_START = 2
-V0_HEAD = 4
+V0_HEAD = 3
 V00_AT = 1
-V00_PLAN = ((0, "V"), (0, "V"), (0, "V"), (0, "V"))
-FILL_ON = "AAV"
-PREP_ON = "AAVAVAVA"
-V0_PLAN = ((0, "V"), (0, "P"), (1, "L"), (1, "P"), 2)
-V1_PLAN = ((2, "P"), (2, "P"), (3, "P"), (4, "P"), (4, "P"), (5, "P"), (6, "P"), (6, "P"), 5, 7)
-CAST_PLAN = (((7, "P"), (8, "P"), (9, "P"), (10, "P"), 11), ((9, "V"), (10, "V"), (11, "P"), (11, "L"), 12), ((12, "P"), (13, "P"), (13, "V"), (13, "L"), 14))
+V00_PLAN = ((2, "V"), (0, "P"), (2, "P"), (0, "V"))
+FILL_ON = "AAA"
+PREP_ON = "AAAAAVAA"
+V0_PLAN = ((0, "L"), (0, "V"), (0, "P"), (1, "L"), 2)
+V1_PLAN = ((1, "L"), (3, "P"), (5, "P"), (1, "P"), (8, "L"), (5, "V"), (6, "P"), (8, "P"), 9, 9)
+CAST_PLAN = (((7, "P"), (9, "A"), (9, "L"), (10, "P"), 13), ((10, "V"), (12, "V"), (10, "L"), (11, "V"), 14), ((13, "L"), (14, "A"), (14, "A"), (14, "A"), 15))
 
 
 def tile_fourierkolmogorovarnoldattention_x1_kernel(tc, q, k, v, ca, cb, g, out_0, out_1, out_2):
@@ -233,7 +235,7 @@ def tile_fourierkolmogorovarnoldattention_x1_kernel(tc, q, k, v, ca, cb, g, out_
             h = head(i)
             y_t[i] = work.tile([P, 1024], F32, name="y", tag="y")
             if MODES[i] in "BC":
-                for lo, hi in (U_PARTS if MODES[i] == "C" else ((0, 1024),)):
+                for lo, hi in Y_PARTS:
                     nc.scalar.activation(out=y_t[i][:, lo:hi], in_=u_t[i][:, lo:hi], func=ACT.Square, bias=nus[:, h:h + 1])
             else:
                 stt(y_t[i][:], u_t[i][:], c_a[:, h:h + 1], add, u_t[i][:], mul)
@@ -284,11 +286,14 @@ def tile_fourierkolmogorovarnoldattention_x1_kernel(tc, q, k, v, ca, cb, g, out_
                                     rhs=codes[("v", h)][:, vcols].bitcast(FP8X4), rhs_scale=scales[("v", h)][:, vcols],
                                     start=(kk == 0), stop=(kk == 1))
 
-        def result(i, bank, lo, hi):
+        def result(i, bank, lo, hi, eng="A"):
             grp, t = divmod(i, PACK)
             if grp not in o_sb:
                 o_sb[grp] = work.tile([P, PACK, DV], F32, name="o_sb", tag="o_sb", bufs=3)
-            nc.scalar.mul(out=o_sb[grp][:, t, lo:hi], in_=bank[:, lo:hi], mul=1.0 / math.sqrt(TK))
+            if eng == "A":
+                nc.scalar.mul(out=o_sb[grp][:, t, lo:hi], in_=bank[:, lo:hi], mul=1.0 / math.sqrt(TK))
+            else:
+                ts(o_sb[grp][:, t, lo:hi], bank[:, lo:hi], 1.0 / math.sqrt(TK), mul)
 
         def store_result(i, count=1):
             grp, t = divmod(i, PACK)
@@ -622,10 +627,11 @@ def tile_fourierkolmogorovarnoldattention_x1_kernel(tc, q, k, v, ca, cb, g, out_
                 weighted_sum(i - 1, out_bank(i - 1), 0, DV)
             if i in jobs:
                 prep_transpose(jobs[i])
-            if i >= AV_START:
+            if i >= AV_START and EVAC_ON[i] == "A":
                 result(i - 1, o_ps[i - 1], 0, DV)
                 store_result(i - 1)
-            cubic_second(i, 0, 1024)
+            for lo, hi in (Y_PARTS if MODES[i] == "C" else ((0, 1024),)):
+                cubic_second(i, lo, hi)
             turn(i, True)
             if i > 8:
                 keep_warm(WARM[0])
@@ -640,6 +646,9 @@ def tile_fourierkolmogorovarnoldattention_x1_kernel(tc, q, k, v, ca, cb, g, out_
             whole_turns(i + 2, 1)
             fraction(i + 2, 0)
             fraction(i + 2, 1)
+            if i >= AV_START and EVAC_ON[i] == "V":
+                result(i - 1, o_ps[i - 1], 0, DV, "V")
+                store_result(i - 1)
             if i in jobs and PREP_ON[i] == "V":
                 prep_copy(jobs[i], "V")
             if live(i + 3):
@@ -679,7 +688,8 @@ def tile_fourierkolmogorovarnoldattention_x1_kernel(tc, q, k, v, ca, cb, g, out_
         turn(last, True, (1,))
         if not AV_EARLY:
             weighted_sum(last - 1, out_bank(last - 1), 0, DV)
-        result(last - 1, o_ps[last - 1], 0, DV)
+        if EVAC_ON[last] == "A":
+            result(last - 1, o_ps[last - 1], 0, DV)
         extra(last - 1, "V")
         gain(last, 0)
         gain(last, 1)
@@ -690,6 +700,8 @@ def tile_fourierkolmogorovarnoldattention_x1_kernel(tc, q, k, v, ca, cb, g, out_
         quantize_ag(last, 1, 2)
         weighted_sum(last, out_bank(last), 0, 256, (1,))
         weighted_sum(last, other, 256, DV, (1,))
+        if EVAC_ON[last] == "V":
+            result(last - 1, o_ps[last - 1], 0, DV, "V")
         extra(last, "V")
         result(last, o_ps[last], 0, 256)
         round_result(3, 0, 256, "V")

import math
from contextlib import ExitStack

import concourse.mybir as mybir
from concourse.masks import make_identity

H, TQ, TK, E, DV = 2, 1024, 1024, 512, 512
FLOPS = 2 * H * TQ * TK * (E + DV)

F32 = mybir.dt.float32
BF16 = mybir.dt.bfloat16
I32 = mybir.dt.int32
U32 = mybir.dt.uint32
U8 = mybir.dt.uint8
FP8X4 = mybir.dt.float8_e4m3fn_x4
ALU = mybir.AluOpType
ACT = mybir.ActivationFunctionType
AX = mybir.AxisListType

P = 128
PACK = 4
GROUP = P * PACK
UNITS = H * TQ // P
PI = math.pi
TURNS = 1.0 / (2.0 * PI * math.sqrt(E))
TINY = 1e-37
MODES = "ACCCCCCCCCCCCCDA"
U_PARTS = ((0, 1024),)
WARM = (0, 0, 0, 0, 0)
AV_EARLY = 0
Y_PARTS = ((0, 512), (512, 1024))
EVAC_ON = "AAAVAAAAAVAAAAAA"
AV_START = 2
V0_HEAD = 3
V00_AT = 1
V00_PLAN = ((2, "V"), (0, "P"), (2, "P"), (0, "V"))
FILL_ON = "AAA"
PREP_ON = "AAAAAVAA"
V0_PLAN = ((0, "L"), (0, "V"), (0, "P"), (1, "L"), 2)
V1_PLAN = ((1, "L"), (3, "P"), (5, "P"), (1, "P"), (8, "L"), (5, "V"), (6, "P"), (8, "P"), 9, 9)
CAST_PLAN = (((7, "P"), (9, "A"), (9, "L"), (10, "P"), 13), ((10, "V"), (12, "V"), (10, "L"), (11, "V"), 14), ((13, "L"), (14, "A"), (14, "A"), (14, "A"), 15))


def tile_fourierkolmogorovarnoldattention_x1_kernel(tc, q, k, v, ca, cb, g, out_0, out_1, out_2):
    nc = tc.nc
    with ExitStack() as ctx:
        keep = ctx.enter_context(tc.tile_pool(name="keep", bufs=1))
        work = ctx.enter_context(tc.tile_pool(name="work", bufs=2))
        psum = ctx.enter_context(tc.psum_pool(name="psum", bufs=1))
        ctx.enter_context(tc.manual_schedule())

        ca_sb = keep.tile([P, H, 3], BF16, name="ca_sb")
        cb_sb = keep.tile([P, H, 3], BF16, name="cb_sb")
        g_sb = keep.tile([P, H * 2, PACK], BF16, name="g_sb")
        nc.sync.dma_start(out=ca_sb[:].rearrange("p h m -> p (h m)"),
                          in_=ca.rearrange("h m -> (h m)").partition_broadcast(P))
        nc.sync.dma_start(out=cb_sb[:].rearrange("p h m -> p (h m)"),
                          in_=cb.rearrange("h m -> (h m)").partition_broadcast(P))
        raw = {}

        def load(name, src, h, half, lo=0, hi=PACK):
            if lo == 0:
                raw[(name, h, half)] = keep.tile([P, PACK, 512], BF16, name="raw_%s%d%d" % (name, h, half), align_bytes=64)
            rows = src[h, half * GROUP:(half + 1) * GROUP, :].rearrange("(p j) e -> p j e", j=PACK)
            nc.sync.dma_start(out=raw[(name, h, half)][:, lo:hi, :], in_=rows[:, lo:hi, :])

        load("k", k, 0, 0, 0, 2)
        load("k", k, 0, 0, 2, 4)
        load("q", q, 0, 0, 0, 2)
        load("k", k, 0, 1)
        load("q", q, 0, 0, 2, 4)
        load("v", v, 0, 0)
        nc.sync.dma_start(out=g_sb[:], in_=g.rearrange("h (kk p j) -> p (h kk) j", p=P, j=PACK))
        load("q", q, 0, 1)
        load("v", v, 0, 1)
        load("k", k, 1, 0)
        load("v", v, 1, 0)
        load("k", k, 1, 1)
        load("v", v, 1, 1)
        load("q", q, 1, 0)
        load("q", q, 1, 1)

        ident = keep.tile([P, P], F32, name="ident")
        make_identity(nc, ident[:])
        half_t = keep.tile([P, H], F32, name="half_t")
        nc.gpsimd.memset(half_t[:], 0.5)

        codes = {}
        scales = {}
        for name in ("q", "k", "v"):
            for h in range(H):
                codes[(name, h)] = keep.tile([P, 1024], U32, name="codes_%s%d" % (name, h), align_bytes=64)
                scales[(name, h)] = keep.tile([P, 1024], U8, name="scales_%s%d" % (name, h), align_bytes=64)

        def copy(eng, out, in_):
            if eng in "AL":
                nc.scalar.copy(out=out, in_=in_)
            elif eng == "V":
                nc.vector.tensor_copy(out=out, in_=in_)
            else:
                nc.gpsimd.tensor_scalar(out=out, in0=in_, scalar1=1.0, scalar2=0.0, op0=ALU.mult, op1=ALU.add)

        turned = {}
        grouped = {}

        def prep_transpose(job, tag="xt", bufs=2):
            name, h, b = job
            xt = psum.tile([P, 2, 2, P], F32, name="xt", tag=tag, bufs=bufs)
            for s in range(2):
                words = raw[(name, h, b // 2)][:, 2 * (b % 2) + s, :].bitcast(F32)
                for u in range(2):
                    nc.tensor.transpose(xt[:, s, u, :], words[:, u:256:2], ident[:])
            turned[job] = xt

        def prep_copy(job, eng):
            t = work.tile([P, 1024], BF16, name="grouped", tag="grouped", bufs=4, align_bytes=64)
            copy(eng, t[:].bitcast(F32).rearrange("p (s r u) -> p s r u", s=2, u=2),
                 turned[job][:].rearrange("p s u r -> p s r u"))
            grouped[job] = t

        def prep_quantize(job):
            name, h, b = job
            cols = slice(256 * b, 256 * (b + 1))
            nc.vector.quantize_mx(out=codes[(name, h)][:, cols].bitcast(FP8X4), scales=scales[(name, h)][:, cols],
                                  in_=grouped[job][:])

        def v_interleave(h, kk, part, eng):
            if ("v", h, kk) not in grouped:
                grouped[("v", h, kk)] = work.tile([P, 512, PACK], BF16, name="vgrouped", tag="vgrouped", align_bytes=64)
            cols = slice(128 * part, 128 * (part + 1))
            copy(eng, grouped[("v", h, kk)][:, cols, :], raw[("v", h, kk)][:].rearrange("p j d -> p d j")[:, cols, :])

        def v_quantize(h, kk):
            cols = slice(512 * kk, 512 * (kk + 1))
            nc.vector.quantize_mx(out=codes[("v", h)][:, cols].bitcast(FP8X4), scales=scales[("v", h)][:, cols],
                                  in_=grouped[("v", h, kk)][:].rearrange("p d j -> p (d j)"))

        def small(name, *shape):
            return keep.tile([P] + list(shape), F32, name=name)

        def tt(out, a, b, op):
            nc.vector.tensor_tensor(out=out, in0=a, in1=b, op=op)

        def ts(out, a, s1, op0, s2=None, op1=None):
            if op1 is None:
                nc.vector.tensor_scalar(out=out, in0=a, scalar1=s1, scalar2=None, op0=op0)
            else:
                nc.vector.tensor_scalar(out=out, in0=a, scalar1=s1, scalar2=s2, op0=op0, op1=op1)

        def stt(out, a, s, op0, b, op1):
            nc.vector.scalar_tensor_tensor(out=out, in0=a, scalar=s, in1=b, op0=op0, op1=op1)

        def sine(out, a, scale, bias=None):
            if bias is None:
                nc.scalar.activation(out=out, in_=a, func=ACT.Sin, scale=scale)
            else:
                nc.scalar.activation(out=out, in_=a, func=ACT.Sin, scale=scale, bias=bias)

        mul, add, sub, mx = ALU.mult, ALU.add, ALU.subtract, ALU.max
        al = small("al", H)
        be = small("be", H)
        nus = small("nus", H)
        nk = small("nk", H)
        c_a = small("c_a", H)
        c_b = small("c_b", H)
        c_e = small("c_e", H)
        c_e2 = small("c_e2", H)
        xb = small("xb", H)
        psit = small("psit", H)
        psir = small("psir", H)
        gk = small("gk", H * 2, 1, PACK)

        s_ps, whole_t, frac, x_t, u_t, y_t, tb_t, ta_t, z_ps, ag_t, agq, o_ps, o_sb, o_bf, o_q = ({} for n in range(15))

        def head(i):
            return i // 8

        def scores(i, kk):
            h = head(i)
            qcols = slice(P * (i % 8), P * (i % 8 + 1))
            bank = psum.tile([P, 512], F32, name="s_ps", tag="s%d" % kk)
            kcols = slice(512 * kk, 512 * (kk + 1))
            nc.tensor.matmul_mx(out=bank[:], lhsT=codes[("q", h)][:, qcols].bitcast(FP8X4),
                                lhsT_scale=scales[("q", h)][:, qcols],
                                rhs=codes[("k", h)][:, kcols].bitcast(FP8X4), rhs_scale=scales[("k", h)][:, kcols],
                                start=True, stop=True)
            s_ps[(i, kk)] = bank

        def out_bank(i):
            if i not in o_ps:
                o_ps[i] = psum.tile([P, DV], F32, name="o_ps", tag="o", bufs=2)
            return o_ps[i]

        def keep_warm(n):
            for rep in range(n):
                spare = psum.tile([P, 512], F32, name="spare", tag="xt", bufs=2)
                nc.tensor.matmul_mx(out=spare[:], lhsT=codes[("k", 0)][:, 0:P].bitcast(FP8X4),
                                    lhsT_scale=scales[("k", 0)][:, 0:P],
                                    rhs=codes[("k", 0)][:, 0:512].bitcast(FP8X4), rhs_scale=scales[("k", 0)][:, 0:512],
                                    start=True, stop=True)

        def whole_turns(i, kk):
            h = head(i)
            if kk == 0:
                whole_t[i] = work.tile([P, 2, 512], I32, name="whole", tag="whole")
            ts(whole_t[i][:, kk, :], s_ps[(i, kk)][:], TURNS, mul, psit[:, h:h + 1], add)

        def fraction(i, kk):
            if kk == 0:
                frac[i] = work.tile([P, 2, 512], F32, name="frac", tag="frac")
            stt(frac[i][:, kk, :], s_ps[(i, kk)][:], TURNS, mul, whole_t[i][:, kk, :], sub)

        def half_sine(i):
            h = head(i)
            x_t[i] = work.tile([P, 1024], F32, name="x", tag="x")
            sine(x_t[i][:], frac[i][:].rearrange("p a n -> p (a n)"), PI, xb[:, h:h + 1])

        def square_x(i):
            u_t[i] = work.tile([P, 1024], F32, name="u", tag="u_last" if i == UNITS - 1 else "u", bufs=1)
            if MODES[i] in "CD":
                for lo, hi in U_PARTS:
                    nc.gpsimd.tensor_tensor(out=u_t[i][:, lo:hi], in0=x_t[i][:, lo:hi], in1=x_t[i][:, lo:hi], op=mul)
            else:
                nc.scalar.activation(out=u_t[i][:], in_=x_t[i][:], func=ACT.Square)

        def square_term(i):
            h = head(i)
            sn = work.tile([P, 1024], F32, name="sn", tag="sn")
            tb_t[i] = work.tile([P, 1024], F32, name="tb", tag="tb")
            sine(sn[:], frac[i][:].rearrange("p a n -> p (a n)"), 2 * PI, psir[:, h:h + 1])
            return lambda: nc.scalar.activation(out=tb_t[i][:], in_=sn[:], func=ACT.Square, scale=al[:, h:h + 1],
                                                bias=be[:, h:h + 1])

        def cubic_first(i):
            h = head(i)
            y_t[i] = work.tile([P, 1024], F32, name="y", tag="y")
            if MODES[i] in "BC":
                for lo, hi in Y_PARTS:
                    nc.scalar.activation(out=y_t[i][:, lo:hi], in_=u_t[i][:, lo:hi], func=ACT.Square, bias=nus[:, h:h + 1])
            else:
                stt(y_t[i][:], u_t[i][:], c_a[:, h:h + 1], add, u_t[i][:], mul)

        def cubic_second(i, lo, hi):
            h = head(i)
            if lo == 0:
                ta_t[i] = work.tile([P, 1024], F32, name="ta", tag="ta")
            if MODES[i] in "BC":
                stt(ta_t[i][:, lo:hi], u_t[i][:, lo:hi], nk[:, h:h + 1], add, y_t[i][:, lo:hi], mul)
            else:
                stt(ta_t[i][:, lo:hi], y_t[i][:, lo:hi], c_b[:, h:h + 1], add, u_t[i][:, lo:hi], mul)

        def turn(i, second, halves=(0, 1)):
            for kk in halves:
                if not second:
                    z_ps[(i, kk)] = psum.tile([P, PACK, P], F32, name="z_ps", tag=("s%d" if i == UNITS - 1 else "z%d") % kk)
                src = ta_t[i] if second else tb_t[i]
                for j in range(PACK):
                    cols = slice(512 * kk + P * j, 512 * kk + P * (j + 1))
                    nc.tensor.matmul(out=z_ps[(i, kk)][:, j, :], lhsT=src[:, cols], rhs=ident[:],
                                     start=(not second and j == 0), stop=(second and j == PACK - 1), is_transpose=True)

        def gain(i, kk):
            h = head(i)
            if kk == 0:
                ag_t[i] = work.tile([P, 2, P, PACK], BF16, name="ag", tag="ag", align_bytes=64)
            const = c_e2 if MODES[i] in "BC" else c_e
            stt(ag_t[i][:, kk, :, :], z_ps[(i, kk)][:].rearrange("p j n -> p n j"), const[:, h:h + 1], add,
                gk[:, 2 * h + kk, :, :].to_broadcast([P, P, PACK]), mul)

        def quantize_ag(i, lo, hi):
            if lo == 0:
                c = work.tile([P, 2 * P], U32, name="ag_codes", tag="ag_codes", bufs=AV_START + 1, align_bytes=64)
                s = work.tile([P, 2 * P], U8, name="ag_scales", tag="ag_scales", bufs=AV_START + 1, align_bytes=64)
                agq[i] = (c, s)
            c, s = agq[i]
            nc.vector.quantize_mx(out=c[:, P * lo:P * hi].bitcast(FP8X4), scales=s[:, P * lo:P * hi],
                                  in_=ag_t[i][:, lo:hi, :, :].rearrange("p a n j -> p (a n j)"))

        def weighted_sum(i, bank, lo, hi, halves=(0, 1)):
            h = head(i)
            c, s = agq[i]
            for kk in halves:
                acols = slice(P * kk, P * (kk + 1))
                vcols = slice(512 * kk + lo, 512 * kk + hi)
                nc.tensor.matmul_mx(out=bank[:, lo:hi], lhsT=c[:, acols].bitcast(FP8X4), lhsT_scale=s[:, acols],
                                    rhs=codes[("v", h)][:, vcols].bitcast(FP8X4), rhs_scale=scales[("v", h)][:, vcols],
                                    start=(kk == 0), stop=(kk == 1))

        def result(i, bank, lo, hi, eng="A"):
            grp, t = divmod(i, PACK)
            if grp not in o_sb:
                o_sb[grp] = work.tile([P, PACK, DV], F32, name="o_sb", tag="o_sb", bufs=3)
            if eng == "A":
                nc.scalar.mul(out=o_sb[grp][:, t, lo:hi], in_=bank[:, lo:hi], mul=1.0 / math.sqrt(TK))
            else:
                ts(o_sb[grp][:, t, lo:hi], bank[:, lo:hi], 1.0 / math.sqrt(TK), mul)

        def store_result(i, count=1):
            grp, t = divmod(i, PACK)
            h, gq = divmod(grp, 2)
            rows = out_0[h, GROUP * gq:GROUP * (gq + 1), :].rearrange("(p t) d -> p t d", t=PACK)
            nc.sync.dma_start(out=rows[:, t:t + count, :], in_=o_sb[grp][:, t:t + count, :])

        def round_result(grp, lo, hi, eng):
            if grp not in o_bf:
                o_bf[grp] = work.tile([P, DV, PACK], BF16, name="o_bf", tag="o_bf", align_bytes=64)
            src = o_sb[grp][:].rearrange("p t d -> p d t")
            copy(eng, o_bf[grp][:, lo:hi, :], src[:, lo:hi, :])

        def planes(grp, lo, hi):
            if grp not in o_q:
                c = work.tile([P, DV], U32, name="o_codes", tag="o_codes", align_bytes=64)
                s = work.tile([P, DV], U8, name="o_scales", tag="o_scales", align_bytes=64)
                o_q[grp] = (c, s)
            c, s = o_q[grp]
            nc.vector.quantize_mx(out=c[:, lo:hi].bitcast(FP8X4), scales=s[:, lo:hi],
                                  in_=o_bf[grp][:, lo:hi, :].rearrange("p d t -> p (d t)"))

        def store_planes(grp, engines):
            h, gq = divmod(grp, 2)
            c, s = o_q[grp]
            cols = slice(DV * h, DV * (h + 1))
            nc.sync.dma_start(out=out_1[gq, :, cols, :].rearrange("p m t -> p (m t)").bitcast(I32), in_=c[:].bitcast(I32))
            for quad in range(4):
                engines[quad].dma_start(out=out_2[gq, 4 * quad:4 * quad + 4, cols].bitcast(I32),
                                        in_=s[32 * quad:32 * quad + 4, :].bitcast(I32))

        def whole_planes(grp):
            planes(grp, 0, DV)
            store_planes(grp, [nc.sync] * 4)

        first = [("k", 0, 0), ("k", 0, 1), ("q", 0, 0), ("k", 0, 2), ("k", 0, 3), ("q", 0, 1)]
        prep_transpose(first[0])
        prep_transpose(first[1])
        prep_transpose(first[2], "o", 2)
        prep_transpose(first[3], "o", 2)
        prep_transpose(first[4], "z0", 1)
        absa = small("absa", H, 3)
        absb = small("absb", H, 3)
        m3 = small("m3", H)
        im3 = small("im3", H)
        r = small("r", 3, H)
        cs = small("cs", 2, H)
        flat_a = ca_sb[:].rearrange("p h m -> p (h m)")
        flat_b = cb_sb[:].rearrange("p h m -> p (h m)")
        stt(absa[:].rearrange("p h m -> p (h m)"), flat_a, -1.0, mul, flat_a, mx)
        stt(absb[:].rearrange("p h m -> p (h m)"), flat_b, -1.0, mul, flat_b, mx)
        sig0 = small("sig0", H)
        ts(sig0[:], cb_sb[:, :, 2], 0.0, ALU.is_le, 2.0, mul)
        stt(m3[:], absb[:, :, 2], TINY, mx, absa[:, :, 2], add)
        sig = small("sig", H, 1)
        ts(sig[:, :, 0], sig0[:], -1.0, add)
        absab = small("absab", H, 3)
        tt(absab[:], absa[:], absb[:], add)
        nc.vector.reciprocal(out=im3[:], in_=m3[:])
        larger = small("larger", H, 3)
        tt(larger[:], absa[:], absb[:], mx)
        total = small("total", H)
        nc.vector.tensor_reduce(out=total[:], in_=absab[:], axis=AX.X, op=add)
        stt(r[:, 0, :], ca_sb[:, :, 2], -1.0, mul, im3[:], mul)
        stt(r[:, 1, :], absb[:, :, 2], TINY, mx, im3[:], mul)
        sine(cs[:], r[:, 0:2, :], PI / 2)
        stt(r[:, 2, :], ca_sb[:, :, 2], -1.0, mul, im3[:], mul)
        prep_copy(first[0], "A")
        prep_copy(first[1], "A")
        base = small("base", H)
        ts(base[:], r[:, 0, :], -PI / 6, mul, PI / 6, add)
        ab = small("ab", 2, H, 2)
        ba = small("ba", 2, H, 2)
        nc.vector.tensor_copy(out=ab[:, 0, :, :], in_=ca_sb[:, :, 0:2])
        nc.vector.tensor_copy(out=ab[:, 1, :, :], in_=cb_sb[:, :, 0:2])
        tt(ba[:, 0, :, :], cb_sb[:, :, 0:2], sig[:].to_broadcast([P, H, 2]), mul)
        stt(ba[:, 1, :, :], ca_sb[:, :, 0:2], -1.0, mul, sig[:].to_broadcast([P, H, 2]), mul)
        pr1 = small("pr1", 2, H)
        pr2 = small("pr2", 2, H)
        tt(pr1[:], r[:, 0:2, :], cs[:], mul)
        tt(pr2[:], r[:, 1:3, :], cs[:], mul)
        floor = small("floor", H)
        ts(floor[:], total[:], 2.0 ** -40, mul)
        den = small("den", H)
        num = small("num", H)
        tt(den[:], pr1[:, 0, :], pr1[:, 1, :], add)
        tt(num[:], pr2[:, 0, :], pr2[:, 1, :], sub)
        bound = small("bound", H, 3)
        stt(bound[:], absab[:], 0.7072, mul, larger[:], add)
        iden = small("iden", H)
        nc.vector.reciprocal(out=iden[:], in_=den[:])
        dm = small("dm", H)
        stt(dm[:], den[:], 32.0, mul, m3[:], mul)
        c00 = small("c00", H)
        stt(c00[:], bound[:, :, 0], 0.6, mul, bound[:, :, 1], add)
        z = small("z", H)
        tt(z[:], num[:], iden[:], mul)
        c0 = small("c0", H)
        ts(c0[:], c00[:], 0.9205, mul, TINY, mx)
        ic0 = small("ic0", H)
        nc.vector.reciprocal(out=ic0[:], in_=c0[:])
        prep_copy(first[2], "A")
        prep_quantize(first[0])
        w = small("w", H)
        tt(w[:], z[:], z[:], mul)
        z3 = small("z3", H)
        ts(z3[:], z[:], 1.0 / 3.0, mul)
        pa1 = small("pa1", H)
        pb1 = small("pb1", H)
        zw = small("zw", H)
        q1 = small("q1", H)
        ts(pa1[:], w[:], -1.0 / 3.0, mul, 1.0, add)
        ts(pb1[:], w[:], -1.0 / 7.0, mul, 1.0 / 5.0, add)
        tt(zw[:], z3[:], w[:], mul)
        ts(q1[:], w[:], 1.0 / 16.0, mul, -1.0 / 8.0, add)
        pa2 = small("pa2", H)
        zw2 = small("zw2", H)
        q2 = small("q2", H)
        tt(pa2[:], pa1[:], z3[:], mul)
        tt(zw2[:], zw[:], w[:], mul)
        tt(q2[:], q1[:], w[:], mul)
        pa3 = small("pa3", H)
        pb2 = small("pb2", H)
        q3 = small("q3", H)
        tt(pa3[:], pa2[:], base[:], add)
        tt(pb2[:], pb1[:], zw2[:], mul)
        stt(q3[:], q2[:], 0.5, add, w[:], mul)
        prep_quantize(first[1])
        pa = small("pa", H)
        tt(pa[:], pa3[:], pb2[:], add)
        r32 = small("r32", H)
        stt(r32[:], q3[:], 1.0, add, dm[:], mul)
        cosm = small("cosm", 1, H, 2)
        sinm = small("sinm", 1, H, 2)
        sine(cosm[:, 0, :, 0], pa[:], -1.0, PI / 2)
        sine(cosm[:, 0, :, 1], pa[:], -2.0, PI / 2)
        sine(sinm[:, 0, :, 0], pa[:], 1.0)
        sine(sinm[:, 0, :, 1], pa[:], 2.0)
        prep_copy(first[3], "A")
        prep_copy(first[4], "A")
        prep_quantize(first[2])
        scores(0, 0)
        phi = small("phi", H)
        tt(phi[:], pa[:], sig[:, :, 0], mul)
        big_k = small("big_k", H, 1)
        tt(big_k[:, :, 0], r32[:], floor[:], mx)
        phit = small("phit", H)
        ts(phit[:], phi[:], 1.0 / (2 * PI), mul)
        ik = small("ik", H, 1)
        nc.vector.reciprocal(out=ik[:, :, 0], in_=big_k[:, :, 0])
        rc = small("rc", 2, H * 2)
        rs = small("rs", 2, H * 2)
        tt(rc[:], ab[:].rearrange("p a h m -> p a (h m)"),
           cosm[:].rearrange("p a h m -> p a (h m)").to_broadcast([P, 2, H * 2]), mul)
        tt(rs[:], ba[:].rearrange("p a h m -> p a (h m)"),
           sinm[:].rearrange("p a h m -> p a (h m)").to_broadcast([P, 2, H * 2]), mul)
        rot = small("rot", 2, H, 2)
        tt(rot[:].rearrange("p a h m -> p a (h m)"), rc[:], rs[:], add)
        prep_quantize(first[3])
        rho = small("rho", H)
        tt(rho[:], rot[:, 1, :, 1], ic0[:], mul)
        ts(xb[:], phi[:], -0.5, mul)
        ak = small("ak", H, 2)
        tt(ak[:], rot[:, 0, :, :], ik[:].to_broadcast([P, H, 2]), mul)
        nm = small("nm", 2, H)
        tt(nm[:, 1, :], rot[:, 1, :, 0], ik[:, :, 0], mul)
        stt(psit[:], rho[:], 1.0 / 8.0, mul, phit[:], sub)
        ar = small("ar", H)
        stt(ar[:], rho[:], -1.0, mul, rho[:], mx)
        stt(psir[:], rho[:], PI / 4, mul, phi[:], sub)
        prep_quantize(first[4])
        zr = small("zr", H)
        ts(zr[:], ar[:], 1e-4, mx)
        whole_turns(0, 0)
        scores(0, 1)
        prep_transpose(first[5], "z1", 1)
        mk = small("mk", H)
        stt(mk[:], c0[:], 2.0, mul, ik[:, :, 0], mul)
        dn = small("dn", 2, H)
        sd = small("sd", H)
        c2d = small("c2d", H)
        sine(dn[:, 1, :], rho[:], PI / 4, PI / 2)
        sine(sd[:], rho[:], PI / 4)
        sine(c2d[:], ar[:], -PI / 2, PI / 2)
        sine(dn[:, 0, :], zr[:], PI / 2)

        idn = small("idn", 2, H)
        ml = small("ml", 2, H)
        t_a2 = small("t_a2", H)
        t_a1 = small("t_a1", H)
        a2 = small("a2", H)
        a1 = small("a1", H)
        e0 = small("e0", H)
        ial = small("ial", H)
        e1 = small("e1", H)
        be2 = small("be2", H)
        wq = small("wq", H)
        sq16 = small("sq16", H)
        disc = small("disc", H)
        root = small("root", H)
        dd = small("dd", H)
        idd = small("idd", H)
        nus0 = small("nus0", H)
        us2 = small("us2", H)
        e3 = small("e3", H)
        b0 = small("b0", H)
        late = [
            [lambda: tt(nm[:, 0, :], mk[:], zr[:], mul), lambda: nc.vector.reciprocal(out=idn[:], in_=dn[:])],
            [lambda: tt(ml[:], nm[:], idn[:], mul),
             lambda: nc.gpsimd.tensor_tensor(out=al[:], in0=ml[:, 0, :], in1=half_t[:], op=ALU.pow)],
            [lambda: stt(t_a2[:], ml[:, 0, :], 0.5, mul, c2d[:], mul), lambda: tt(t_a1[:], ml[:, 1, :], sd[:], mul)],
            [lambda: tt(a2[:], t_a2[:], ak[:, :, 1], add), lambda: tt(a1[:], ak[:, :, 0], t_a1[:], sub),
             lambda: nc.vector.reciprocal(out=ial[:], in_=al[:])],
            [lambda: ts(wq[:], a1[:], 3.0 / 32.0, add), lambda: stt(sq16[:], a2[:], 16.0, mul, a2[:], mul),
             lambda: stt(be[:], ml[:, 1, :], 0.5, mul, ial[:], mul), lambda: ts(c_a[:], a2[:], 8.0, mul, -1.5, add),
             lambda: stt(b0[:], a2[:], 4.0, mul, a1[:], add)],
            [lambda: stt(disc[:], wq[:], 1.5, mul, sq16[:], add),
             lambda: nc.gpsimd.tensor_tensor(out=root[:], in0=disc[:], in1=half_t[:], op=ALU.pow),
             lambda: stt(e0[:], a2[:], -1.0 / 32.0, add, a1[:], add), lambda: tt(be2[:], be[:], be[:], mul),
             lambda: ts(c_b[:], b0[:], -2.0, mul, 9.0 / 16.0, add)],
            [lambda: stt(e1[:], ml[:, 0, :], -0.5, mul, e0[:], add),
             lambda: tt(gk[:].rearrange("p (h kk) o j -> p h (kk o j)", h=H),
                        g_sb[:].rearrange("p (h kk) j -> p h (kk j)", h=H), big_k[:].to_broadcast([P, H, 2 * PACK]), mul),
             lambda: stt(dd[:], a2[:], 4.0, mul, root[:], add)],
            [lambda: tt(c_e[:], e1[:], be2[:], sub), lambda: nc.vector.reciprocal(out=idd[:], in_=dd[:])],
            [lambda: stt(nus0[:], wq[:], -1.0, mul, idd[:], mul)],
            [lambda: ts(nus[:], nus0[:], -0.5, add)],
            [lambda: stt(nk[:], nus[:], -2.0, mul, c_a[:], add), lambda: tt(us2[:], nus[:], nus[:], mul)],
            [lambda: tt(e3[:], nk[:], us2[:], mul)],
            [lambda: tt(c_e2[:], c_e[:], e3[:], sub)],
        ]

        def constants(n):
            for call in late[n]:
                call()

        jobs = {-2: ("q", 0, 2), -1: ("q", 0, 3), 0: ("k", 1, 0), 1: ("k", 1, 1), 2: ("k", 1, 2), 3: ("k", 1, 3),
                4: ("q", 1, 0), 5: ("q", 1, 1), 6: ("q", 1, 2), 7: ("q", 1, 3)}
        extras = {(i, e): [] for i in range(UNITS + 1) for e in "AVPL"}
        for n in range(4):
            step, eng = V0_PLAN[n]
            extras[(step, eng)].append(lambda n=n, eng=eng: v_interleave(0, 1, n, eng))
        for n in range(V0_HEAD, 4):
            step, eng = V00_PLAN[n]
            extras[(step, eng)].append(lambda n=n, eng=eng: v_interleave(0, 0, n, eng))
        extras[(V0_PLAN[4], "V")].append(lambda: v_quantize(0, 1))
        for n in range(8):
            step, eng = V1_PLAN[n]
            extras[(step, eng)].append(lambda n=n, eng=eng: v_interleave(1, n // 4, n % 4, eng))
        extras[(V1_PLAN[8], "V")].append(lambda: v_quantize(1, 0))
        extras[(V1_PLAN[9], "V")].append(lambda: v_quantize(1, 1))
        for grp in range(3):
            for n in range(4):
                step, eng = CAST_PLAN[grp][n]
                extras[(step, eng)].append(lambda grp=grp, n=n, eng=eng: round_result(grp, n * P, (n + 1) * P, eng))
            extras[(CAST_PLAN[grp][4], "V")].append(lambda grp=grp: whole_planes(grp))

        def extra(i, eng):
            for call in extras[(i, eng)]:
                call()

        def live(i):
            return 0 <= i < UNITS

        def finish_unit(i):
            weighted_sum(i, out_bank(i), 0, DV)
            result(i, o_ps[i], 0, DV)
            store_result(i)

        for n in range(V0_HEAD):
            v_interleave(0, 0, n, "A")
        constants(0)
        fraction(0, 0)
        scores(1, 0)
        constants(1)
        whole_turns(0, 1)
        constants(2)
        prep_copy(first[5], FILL_ON[2])
        fraction(0, 1)
        scores(1, 1)
        prep_transpose(jobs[-2])
        prep_transpose(jobs[-1])
        half_sine(0)
        finish = square_term(0)
        square_x(0)
        constants(3)
        prep_quantize(first[5])
        constants(4)
        finish()
        whole_turns(1, 0)
        constants(5)
        whole_turns(1, 1)
        constants(6)
        fraction(1, 0)
        constants(7)
        fraction(1, 1)
        scores(2, 0)
        scores(2, 1)
        half_sine(1)
        constants(8)
        cubic_first(0)
        constants(9)
        turn(0, False)
        prep_copy(jobs[-2], FILL_ON[0])
        prep_copy(jobs[-1], FILL_ON[1])
        extras[(1, "V")].append(lambda: prep_quantize(jobs[-2]))
        extras[(V00_AT, "V")].append(lambda: v_quantize(0, 0))

        last = UNITS - 1
        for i in range(last - 1):
            finish = square_term(i + 1)
            if i == 1:
                constants(10)
            if i - 1 in jobs and i > 0:
                prep_quantize(jobs[i - 1])
            if i == 2:
                prep_quantize(jobs[-1])
            extra(i, "V")
            if i > 0 and MODES[i] in "AD":
                cubic_first(i)
            if i == 1:
                constants(11)
            if i > 0:
                quantize_ag(i - 1, 0, 2)
            if i == 1:
                constants(12)
            if i == AV_START:
                for n in range(AV_START - 1):
                    finish_unit(n)
            if i >= AV_START:
                weighted_sum(i - 1, out_bank(i - 1), 0, DV)
            if i in jobs:
                prep_transpose(jobs[i])
            if i >= AV_START and EVAC_ON[i] == "A":
                result(i - 1, o_ps[i - 1], 0, DV)
                store_result(i - 1)
            for lo, hi in (Y_PARTS if MODES[i] == "C" else ((0, 1024),)):
                cubic_second(i, lo, hi)
            turn(i, True)
            if i > 8:
                keep_warm(WARM[0])
            if i in jobs and PREP_ON[i] == "A":
                prep_copy(jobs[i], "A")
            extra(i, "A")
            square_x(i + 1)
            extra(i, "P")
            finish()
            extra(i, "L")
            whole_turns(i + 2, 0)
            whole_turns(i + 2, 1)
            fraction(i + 2, 0)
            fraction(i + 2, 1)
            if i >= AV_START and EVAC_ON[i] == "V":
                result(i - 1, o_ps[i - 1], 0, DV, "V")
                store_result(i - 1)
            if i in jobs and PREP_ON[i] == "V":
                prep_copy(jobs[i], "V")
            if live(i + 3):
                scores(i + 3, 0)
                scores(i + 3, 1)
            else:
                keep_warm(WARM[1])
            if MODES[i + 1] in "BC":
                cubic_first(i + 1)
            half_sine(i + 2)
            gain(i, 0)
            gain(i, 1)
            turn(i + 1, False)

        keep_warm(WARM[2])
        square_x(last)
        square_term(last)()
        if MODES[last - 1] in "AD":
            cubic_first(last - 1)
        quantize_ag(last - 2, 0, 2)
        finish_unit(last - 2)
        extra(last - 1, "A")
        cubic_second(last - 1, 0, 1024)
        turn(last - 1, True)
        keep_warm(WARM[3])
        cubic_first(last)
        turn(last, False)
        keep_warm(WARM[4])
        gain(last - 1, 0)
        gain(last - 1, 1)
        cubic_second(last, 0, 512)
        turn(last, True, (0,))
        quantize_ag(last - 1, 0, 2)
        cubic_second(last, 512, 1024)
        if AV_EARLY:
            weighted_sum(last - 1, out_bank(last - 1), 0, DV)
        turn(last, True, (1,))
        if not AV_EARLY:
            weighted_sum(last - 1, out_bank(last - 1), 0, DV)
        if EVAC_ON[last] == "A":
            result(last - 1, o_ps[last - 1], 0, DV)
        extra(last - 1, "V")
        gain(last, 0)
        gain(last, 1)
        other = psum.tile([P, DV], F32, name="o_ps", tag="z0")
        quantize_ag(last, 0, 1)
        weighted_sum(last, out_bank(last), 0, 256, (0,))
        weighted_sum(last, other, 256, DV, (0,))
        quantize_ag(last, 1, 2)
        weighted_sum(last, out_bank(last), 0, 256, (1,))
        weighted_sum(last, other, 256, DV, (1,))
        if EVAC_ON[last] == "V":
            result(last - 1, o_ps[last - 1], 0, DV, "V")
        extra(last, "V")
        result(last, o_ps[last], 0, 256)
        round_result(3, 0, 256, "V")
        result(last, other, 256, DV)
        store_result(last - 1, 2)
        round_result(3, 256, 384, "A")
        round_result(3, 384, DV, "V")
        planes(3, 0, 256)
        planes(3, 256, DV)
        store_planes(3, [nc.scalar, nc.scalar, nc.sync, nc.sync])
